import numpy as np
import ml_dtypes


def mxq(x, axis, fmt="e4m3"):
    dtype, down = {"e4m3": (ml_dtypes.float8_e4m3fn, 7), "e5m2": (ml_dtypes.float8_e5m2, 14)}[fmt]
    v = np.moveaxis(np.asarray(x, np.float32).astype(ml_dtypes.bfloat16).astype(np.float64), axis, -1)
    blocks = v.reshape(v.shape[:-1] + (-1, 32))
    amax = np.abs(blocks).max(-1, keepdims=True)
    byte = np.maximum(np.where(amax > 0, np.frexp(amax)[1] - 1 + 127, 0) - down, 1)
    scale = np.exp2(byte - 127.0)
    codes = (blocks / scale).astype(np.float32).astype(dtype).astype(np.float64)
    return np.moveaxis((codes * scale).reshape(v.shape), -1, axis)


WIDE = False


def mx_kscale(k):
    if not WIDE:
        return np.ones(k)
    levels = np.array([10, -10, 5, -5, 0])
    if k % 512:
        return np.exp2(np.random.permutation(np.resize(levels, k // 32))).repeat(32)
    a = np.empty((k // 512, 16))
    for p in range(k // 512):
        a[p, :8] = np.random.permutation(np.resize(levels, 8))
        for g in range(8):
            far = levels[np.abs(levels - a[p, g]) >= 10]
            a[p, g + 8] = far[np.random.randint(len(far))]
    return np.exp2(a.ravel()).repeat(32)


def f64(x):
    return np.asarray(x).astype(np.float64)


def striped(idx):
    return np.tile(idx.reshape(-1, 16).T, (8, 1)).astype(np.uint16)


def unstriped(offs):
    return offs[:16].T.reshape(-1).astype(np.int64)


def pack_weight(w):
    k, n = w.shape
    w = f64(np.asarray(w, np.float32).astype(ml_dtypes.bfloat16)).reshape(k // 32, 32, n)
    amax = np.abs(w).max(1)
    byte = np.clip(np.where(amax > 0, np.frexp(amax)[1] - 1 + 127 - 7, 1), 1, 254)
    scaled = (w * np.exp2(127.0 - byte)[:, None, :]).reshape(k, n).astype(np.float32)
    words = np.ascontiguousarray(scaled.reshape(k // 512, 128, 4, n).transpose(0, 1, 3, 2)).astype(ml_dtypes.float8_e4m3fn).view(np.uint8)
    return words, np.ascontiguousarray(byte.astype(np.uint8).reshape(k // 512, 16, n))


def unpack_weight(words, scales):
    g, p, n, _ = words.shape
    vals = np.ascontiguousarray(words).view(ml_dtypes.float8_e4m3fn).astype(np.float64) * np.repeat(np.exp2(scales.astype(np.float64) - 127.0), 8, axis=1)[..., None]
    return vals.transpose(0, 1, 3, 2).reshape(g * 512, n)


E2M1 = np.array([0.0, 0.5, 1.0, 1.5, 2.0, 3.0, 4.0, 6.0, -0.0, -0.5, -1.0, -1.5, -2.0, -3.0, -4.0, -6.0])


def pack_fp4(w):
    k, n = w.shape
    w = f64(np.asarray(w, np.float32).astype(ml_dtypes.bfloat16)).reshape(k // 32, 32, n)
    amax = np.abs(w).max(1)
    mant, ex = np.frexp(amax / 6.0)
    byte = np.clip(np.where(amax > 0, np.where(mant > 0.5, ex, ex - 1) + 127, 1), 1, 254)
    scaled = (w * np.exp2(127.0 - byte)[:, None, :]).reshape(k, n).astype(np.float32)
    c = np.ascontiguousarray(scaled.reshape(k // 512, 128, 4, n).transpose(0, 1, 3, 2)).astype(ml_dtypes.float4_e2m1fn).view(np.uint8) & 0xF
    words = (c[..., 0::2] | (c[..., 1::2] << 4)).reshape(k // 512, 128, 2 * n)
    return np.ascontiguousarray(words), np.ascontiguousarray(byte.astype(np.uint8).reshape(k // 512, 16, n))


def unpack_fp4(words, scales):
    g, _, n = scales.shape
    words = np.ascontiguousarray(words).reshape(g, 128, n, 2)
    nib = np.empty((g, 128, n, 4), np.uint8)
    nib[..., 0::2] = words & 0xF
    nib[..., 1::2] = words >> 4
    vals = E2M1[nib] * np.repeat(np.exp2(scales.astype(np.float64) - 127.0), 8, axis=1)[..., None]
    return vals.transpose(0, 1, 3, 2).reshape(g * 512, n)


K, T, S, V, H, N = 512, 4096, 1536, 512, 512, 128


def setup_inputs():
    n = np.random.standard_normal
    s = mx_kscale(K)[:, None]
    u = mx_kscale(H)
    packed_xT = pack_weight(n((K, T)) * s)
    packed_w2 = pack_fp4(n((H, N)) / np.sqrt(2 * H) / u[:, None])
    packed_w3 = pack_fp4(n((H, N)) / np.sqrt(2 * H) / u[:, None])
    return {
        "x_words": packed_xT[0],
        "x_scales": packed_xT[1],
        "w1": (n((K, H)) / np.sqrt(K) / s * u).astype(np.float32),
        "w2_words": packed_w2[0],
        "w2_scales": packed_w2[1],
        "w3_words": packed_w3[0],
        "w3_scales": packed_w3[1],
        "offs": striped(np.random.permutation(T)[:S]),
    }


def reference(x_words, x_scales, w1, w2_words, w2_scales, w3_words, w3_scales, offs):
    xq = unpack_weight(x_words, x_scales)[:, unstriped(offs)]
    h = mxq(f64(w1), 0, "e4m3").T @ xq
    mean = (h[:, :V] + h[:, V:2 * V] + h[:, 2 * V:3 * V]) / 3
    dev = np.sqrt(((h[:, :V] - mean) ** 2 + (h[:, V:2 * V] - mean) ** 2 + (h[:, 2 * V:3 * V] - mean) ** 2) / 3)
    return unpack_fp4(w2_words, w2_scales).T @ mxq(mean, 0, "e4m3") + unpack_fp4(w3_words, w3_scales).T @ mxq(dev, 0, "e4m3")

@@ -1,0 +1,230 @@
+from contextlib import ExitStack
+
+import concourse.mybir as mybir
+
+K, T, S, V, H, N = 512, 4096, 1536, 512, 512, 128
+FLOPS = 2 * K * H * S + 2 * 2 * H * N * V
+
+F32 = mybir.dt.float32
+BF16 = mybir.dt.bfloat16
+I32 = mybir.dt.int32
+U32 = mybir.dt.uint32
+U16 = mybir.dt.uint16
+U8 = mybir.dt.uint8
+FP8X4 = mybir.dt.float8_e4m3fn_x4
+FP4X4 = mybir.dt.float4_e2m1fn_x4
+ACT = mybir.ActivationFunctionType
+ALU = mybir.AluOpType
+
+P = 128
+PACK = 4
+CHUNK = 128
+CHUNKS = V // CHUNK
+W1_PIECES = ((0, 128), (128, 384), (384, 512))
+SQRT_FLOOR = 2.0**-116
+
+
+def tile_picked_statpool_none_p_kernel(
+    tc, x_words, x_scales, w1, w2_words, w2_scales, w3_words, w3_scales, offs, out
+):
+    nc = tc.nc
+    with ExitStack() as ctx:
+        keep = ctx.enter_context(tc.tile_pool(name="keep", bufs=1))
+        work = ctx.enter_context(tc.tile_pool(name="work", bufs=4))
+        psum = ctx.enter_context(tc.psum_pool(name="psum", bufs=2))
+
+        offsets = keep.tile([P, S // 16], U16, name="offsets")
+        xs_table = keep.tile([P, T], U8, name="xs_table", tag="scale_rows", align_bytes=64)
+        nc.vector.memset(xs_table[:].bitcast(I32), 0)
+        warm_in = keep.tile([P, 1], F32, name="warm_in", tag="x_words", align_bytes=64)
+        warm_out = keep.tile([P, 1], F32, name="warm_out", tag="w1_late", align_bytes=64)
+        nc.gpsimd.memset(warm_in[:], 1.0)
+        nc.scalar.activation(warm_out[:], warm_in[:], ACT.Sqrt)
+
+        w1_rows = w1.rearrange("(p j) c -> p j c", j=PACK)
+
+        def load_scale_rows(tile_cols, rows):
+            for quad in range(4):
+                nc.sync.dma_start(
+                    tile_cols[32 * quad : 32 * quad + 4, :].bitcast(I32),
+                    rows[4 * quad : 4 * quad + 4, :].bitcast(I32),
+                )
+
+        early = W1_PIECES[0][1]
+        w1_early = keep.tile([P, PACK * early], F32, name="w1_early", tag="w1_early", align_bytes=64)
+        nc.sync.dma_start(offsets[:], offs)
+        w1_raw = [w1_early[:].rearrange("p (j c) -> p j c", j=PACK)]
+        nc.sync.dma_start(w1_raw[0], w1_rows[:, :, 0:early])
+        load_scale_rows(xs_table[:], x_scales[0])
+        x_table = keep.tile([P, T], I32, name="x_table", tag="x_words", align_bytes=64)
+        nc.sync.dma_start(x_table[:], x_words[0].rearrange("p n t -> p (n t)").bitcast(I32))
+        w1_late = keep.tile([P, PACK * (H - early)], F32, name="w1_late", tag="w1_late", align_bytes=64)
+        for c0, c1 in W1_PIECES[1:]:
+            raw = w1_late[:, PACK * (c0 - early) : PACK * (c1 - early)].rearrange("p (j c) -> p j c", j=PACK)
+            nc.sync.dma_start(raw, w1_rows[:, :, c0:c1])
+            w1_raw.append(raw)
+
+        w1_bf = keep.tile([P, PACK, P, PACK], BF16, name="w1_bf", tag="w1_bf", align_bytes=64)
+        for piece, (c0, c1) in enumerate(W1_PIECES):
+            nc.scalar.copy(
+                w1_bf[:, :, c0 // PACK : c1 // PACK, :].rearrange("p t m j -> p m t j"),
+                w1_raw[piece].rearrange("p j (m t) -> p m t j", t=PACK),
+            )
+        w23_codes = keep.tile([P, 4 * N], U8, name="w23_codes", tag="w1_early", align_bytes=64)
+        w2_codes = w23_codes[:, 0 : 2 * N]
+        w3_codes = w23_codes[:, 2 * N : 4 * N]
+        nc.sync.dma_start(w2_codes.bitcast(I32), w2_words[0].bitcast(I32))
+        nc.sync.dma_start(w3_codes.bitcast(I32), w3_words[0].bitcast(I32))
+
+        cols = V // 16
+        xs = [keep.tile([P, V], U8, name=f"xs{d}", align_bytes=64) for d in range(3)]
+        xw = [keep.tile([P, V], U32, name=f"xw{d}", align_bytes=64) for d in range(2)]
+        for d in range(3):
+            nc.vector.tensor_copy(xs[d][:], xs_table[:].indirect(offsets[:, d * cols : (d + 1) * cols]))
+
+        w23_scales = keep.tile([P, 2 * N], U8, name="w23_scales", tag="scale_rows", align_bytes=64)
+        nc.gpsimd.memset(w23_scales[:], 0)
+        load_scale_rows(w23_scales[:, 0:N], w2_scales[0])
+        load_scale_rows(w23_scales[:, N : 2 * N], w3_scales[0])
+
+        def gather_words(d):
+            nc.vector.tensor_copy(xw[d][:], x_table[:].bitcast(U32).indirect(offsets[:, d * cols : (d + 1) * cols]))
+
+        w1_codes = [keep.tile([P, P], U32, name=f"w1_codes{t}", align_bytes=64) for t in range(PACK)]
+        w1_scales = [keep.tile([P, P], U8, name=f"w1_scales{t}", align_bytes=64) for t in range(PACK)]
+        gather_words(0)
+        gather_words(1)
+        for t in range(PACK):
+            nc.vector.quantize_mx(
+                out=w1_codes[t][:].bitcast(FP8X4),
+                scales=w1_scales[t][:],
+                in_=w1_bf[:, t, :, :].rearrange("p m j -> p (m j)"),
+            )
+        xw.append(keep.tile([P, V], U32, name="xw2", tag="w1_bf", align_bytes=64))
+        gather_words(2)
+
+        def first_product(tag, pieces, k):
+            bank = psum.tile([P, PACK, CHUNK], F32, name=tag)
+            v = slice(k * CHUNK, (k + 1) * CHUNK)
+            for t in range(PACK):
+                for n, d in enumerate(pieces):
+                    nc.tensor.matmul_mx(
+                        out=bank[:, t, :],
+                        lhsT=w1_codes[t][:].bitcast(FP8X4),
+                        lhsT_scale=w1_scales[t][:],
+                        rhs=xw[d][:, v].bitcast(FP8X4),
+                        rhs_scale=xs[d][:, v],
+                        start=(n == 0),
+                        stop=(n == len(pieces) - 1),
+                    )
+            return bank[:].rearrange("p t v -> p v t")
+
+        def woven(tile):
+            return tile[:].rearrange("p (v t) -> p v t", t=PACK)
+
+        W = PACK * CHUNK
+        st = [dict() for k in range(CHUNKS)]
+
+        def stage_a(k):
+            s = st[k]
+            third = work.tile([P, W], F32, name="third")
+            if k == 0:
+                h0 = first_product("h0", (0,), k)
+                nc.scalar.activation(woven(third), h0, ACT.Copy, scale=1.0 / 3.0)
+                s["other"] = first_product("h01", (1,), k)
+            else:
+                h01 = first_product("h01", (0, 1), k)
+                nc.scalar.activation(woven(third), h01, ACT.Copy, scale=1.0 / 3.0)
+                s["other"] = first_product("h0", (0,), k)
+            s["third"] = third
+
+        def halves(k):
+            return (slice(0, CHUNK // 2), slice(CHUNK // 2, CHUNK)) if k in (3,) else (slice(0, CHUNK),)
+
+        def differences(k):
+            s = st[k]
+            q = work.tile([P, W], F32, name="q")
+            r = work.tile([P, W], F32, name="r")
+            if k == 0:
+                pair = work.tile([P, W], F32, name="pair")
+                nc.vector.scalar_tensor_tensor(woven(pair), s["other"], 1.0 / 3.0, woven(s["third"]), ALU.mult, ALU.add)
+                nc.vector.scalar_tensor_tensor(woven(q), s["other"], 1.0 / 3.0, woven(s["third"]), ALU.mult, ALU.subtract)
+            else:
+                pair = s["third"]
+                nc.vector.scalar_tensor_tensor(woven(q), s["other"], 2.0 / 3.0, woven(pair), ALU.mult, ALU.subtract)
+            h2 = first_product("h2", (2,), k)
+            for v in halves(k):
+                nc.vector.scalar_tensor_tensor(woven(r)[:, v], h2[:, v], 2.0 / 3.0, woven(pair)[:, v], ALU.mult, ALU.subtract)
+            s["q"], s["r"], s["h2"], s["pair"] = q, r, h2, pair
+
+        def mean_of(k):
+            s = st[k]
+            mean = work.tile([P, W], BF16, name="mean", align_bytes=64)
+            nc.vector.scalar_tensor_tensor(woven(mean), s["h2"], 1.0 / 3.0, woven(s["pair"]), ALU.mult, ALU.add)
+            s["mean"] = mean
+
+        def variance(k):
+            s = st[k]
+            q2 = work.tile([P, W], F32, name="q2")
+            r2 = work.tile([P, W], F32, name="r2")
+            var = work.tile([P, W], F32, name="var")
+            if k in (0,):
+                nc.gpsimd.tensor_tensor(q2[:], s["q"][:], s["q"][:], ALU.mult)
+            else:
+                nc.scalar.activation(q2[:], s["q"][:], ACT.Square)
+            eng = nc.gpsimd if k in (0, 1, 2) else nc.vector
+            for v in halves(k):
+                nc.scalar.activation(woven(r2)[:, v], woven(s["r"])[:, v], ACT.Square, scale=(1.0 / 3.0) ** 0.5)
+            for v in halves(k):
+                eng.tensor_tensor(woven(var)[:, v], woven(q2)[:, v], woven(r2)[:, v], ALU.add)
+            s["var"] = var
+
+        def deviation(k):
+            s = st[k]
+            dev = work.tile([P, W], BF16, name="dev", align_bytes=64)
+            for v in halves(k):
+                nc.scalar.activation(woven(dev)[:, v], woven(s["var"])[:, v], ACT.Sqrt, scale=1.5, bias=SQRT_FLOOR)
+            s["dev"] = dev
+
+        def quantize(values, name):
+            codes = work.tile([P, CHUNK], U32, name=name + "_codes", align_bytes=64)
+            scales = work.tile([P, CHUNK], U8, name=name + "_scales", align_bytes=64)
+            nc.vector.quantize_mx(out=codes[:].bitcast(FP8X4), scales=scales[:], in_=values[:])
+            return codes, scales
+
+        def second_product(k):
+            s = st[k]
+            mean_q = quantize(s["mean"], "mean")
+            dev_q = quantize(s["dev"], "dev")
+            acc = psum.tile([P, CHUNK], F32, name="acc")
+            for n, (codes, (vals, scales)) in enumerate(((w2_codes, mean_q), (w3_codes, dev_q))):
+                nc.tensor.matmul_mx(
+                    out=acc[:],
+                    lhsT=codes.bitcast(FP4X4),
+                    lhsT_scale=w23_scales[:, n * N : (n + 1) * N],
+                    rhs=vals[:].bitcast(FP8X4),
+                    rhs_scale=scales[:],
+                    start=(n == 0),
+                    stop=(n == 1),
+                )
+            res = work.tile([P, CHUNK], F32, name="res")
+            nc.scalar.copy(res[:], acc[:])
+            nc.sync.dma_start(out[:, k * CHUNK : (k + 1) * CHUNK], res[:])
+
+        last = CHUNKS - 1
+        stage_a(0)
+        for k in range(CHUNKS):
+            if k < last:
+                stage_a(k + 1)
+            differences(k)
+            if 0 < k:
+                mean_of(k - 1) if k == last else None
+            if k < last - 1:
+                mean_of(k)
+            variance(k)
+            if k > 0:
+                deviation(k - 1)
+        mean_of(last)
+        deviation(last)
+        for k in range(CHUNKS):
+            second_product(k)

@@ -20,7 +20,7 @@ P = 128
 PACK = 4
 CHUNK = 128
 CHUNKS = V // CHUNK
-W1_PIECES = ((0, 128), (128, 384), (384, 512))
+W1_PIECES = ()
 SQRT_FLOOR = 2.0**-116
 
 
@@ -44,31 +44,23 @@ def tile_picked_statpool_none_p_kernel(
         w1_rows = w1.rearrange("(p j) c -> p j c", j=PACK)
 
         def load_scale_rows(tile_cols, rows):
-            for quad in range(4):
-                nc.sync.dma_start(
-                    tile_cols[32 * quad : 32 * quad + 4, :].bitcast(I32),
-                    rows[4 * quad : 4 * quad + 4, :].bitcast(I32),
-                )
+            for r in range(4):
+                nc.sync.dma_start(tile_cols[r:P:32, :].bitcast(I32), rows[r:16:4, :].bitcast(I32))
 
-        early = W1_PIECES[0][1]
-        w1_early = keep.tile([P, PACK * early], F32, name="w1_early", tag="w1_early", align_bytes=64)
+        w1_early = keep.tile([P, PACK, H // 2], F32, name="w1_early", tag="w1_early", align_bytes=64)
         nc.sync.dma_start(offsets[:], offs)
-        w1_raw = [w1_early[:].rearrange("p (j c) -> p j c", j=PACK)]
-        nc.sync.dma_start(w1_raw[0], w1_rows[:, :, 0:early])
+        nc.sync.dma_start(w1_early[:], w1_rows[:, :, 0 : H // 2])
         load_scale_rows(xs_table[:], x_scales[0])
+        w1_late = keep.tile([P, PACK, H // 2], F32, name="w1_late", tag="w1_late", align_bytes=64)
         x_table = keep.tile([P, T], I32, name="x_table", tag="x_words", align_bytes=64)
+        nc.sync.dma_start(w1_late[:], w1_rows[:, :, H // 2 : H])
         nc.sync.dma_start(x_table[:], x_words[0].rearrange("p n t -> p (n t)").bitcast(I32))
-        w1_late = keep.tile([P, PACK * (H - early)], F32, name="w1_late", tag="w1_late", align_bytes=64)
-        for c0, c1 in W1_PIECES[1:]:
-            raw = w1_late[:, PACK * (c0 - early) : PACK * (c1 - early)].rearrange("p (j c) -> p j c", j=PACK)
-            nc.sync.dma_start(raw, w1_rows[:, :, c0:c1])
-            w1_raw.append(raw)
 
         w1_bf = keep.tile([P, PACK, P, PACK], BF16, name="w1_bf", tag="w1_bf", align_bytes=64)
-        for piece, (c0, c1) in enumerate(W1_PIECES):
+        for half, raw in enumerate((w1_early, w1_late)):
             nc.scalar.copy(
-                w1_bf[:, :, c0 // PACK : c1 // PACK, :].rearrange("p t m j -> p m t j"),
-                w1_raw[piece].rearrange("p j (m t) -> p m t j", t=PACK),
+                w1_bf[:, :, half * P // 2 : (half + 1) * P // 2, :].rearrange("p t m j -> p m t j"),
+                raw[:].rearrange("p j (m t) -> p m t j", t=PACK),
             )
         w23_codes = keep.tile([P, 4 * N], U8, name="w23_codes", tag="w1_early", align_bytes=64)
         w2_codes = w23_codes[:, 0 : 2 * N]
@@ -77,31 +69,28 @@ def tile_picked_statpool_none_p_kernel(
         nc.sync.dma_start(w3_codes.bitcast(I32), w3_words[0].bitcast(I32))
 
         cols = V // 16
-        xs = [keep.tile([P, V], U8, name=f"xs{d}", align_bytes=64) for d in range(3)]
-        xw = [keep.tile([P, V], U32, name=f"xw{d}", align_bytes=64) for d in range(2)]
-        for d in range(3):
-            nc.vector.tensor_copy(xs[d][:], xs_table[:].indirect(offsets[:, d * cols : (d + 1) * cols]))
+        xs_all = keep.tile([P, S], U8, name="xs_all", align_bytes=64)
+        xs = [xs_all[:, d * V : (d + 1) * V] for d in range(3)]
+        xw = [keep.tile([P, V], U32, name=f"xw{d}", align_bytes=64) for d in range(3)]
+        nc.vector.tensor_copy(xs_all[:], xs_table[:].indirect(offsets[:]))
 
         w23_scales = keep.tile([P, 2 * N], U8, name="w23_scales", tag="scale_rows", align_bytes=64)
-        nc.gpsimd.memset(w23_scales[:], 0)
+        nc.gpsimd.memset(w23_scales[:].bitcast(I32), 0)
         load_scale_rows(w23_scales[:, 0:N], w2_scales[0])
         load_scale_rows(w23_scales[:, N : 2 * N], w3_scales[0])
 
         def gather_words(d):
             nc.vector.tensor_copy(xw[d][:], x_table[:].bitcast(U32).indirect(offsets[:, d * cols : (d + 1) * cols]))
 
-        w1_codes = [keep.tile([P, P], U32, name=f"w1_codes{t}", align_bytes=64) for t in range(PACK)]
-        w1_scales = [keep.tile([P, P], U8, name=f"w1_scales{t}", align_bytes=64) for t in range(PACK)]
-        gather_words(0)
-        gather_words(1)
-        for t in range(PACK):
-            nc.vector.quantize_mx(
-                out=w1_codes[t][:].bitcast(FP8X4),
-                scales=w1_scales[t][:],
-                in_=w1_bf[:, t, :, :].rearrange("p m j -> p (m j)"),
-            )
-        xw.append(keep.tile([P, V], U32, name="xw2", tag="w1_bf", align_bytes=64))
-        gather_words(2)
+        w1_codes = keep.tile([P, H], U32, name="w1_codes", align_bytes=64)
+        w1_scales = keep.tile([P, H], U8, name="w1_scales", align_bytes=64)
+        nc.vector.quantize_mx(
+            out=w1_codes[:].bitcast(FP8X4),
+            scales=w1_scales[:],
+            in_=w1_bf[:].rearrange("p t m j -> p (t m j)"),
+        )
+        for d in range(3):
+            gather_words(d)
 
         def first_product(tag, pieces, k):
             bank = psum.tile([P, PACK, CHUNK], F32, name=tag)
@@ -110,8 +99,8 @@ def tile_picked_statpool_none_p_kernel(
                 for n, d in enumerate(pieces):
                     nc.tensor.matmul_mx(
                         out=bank[:, t, :],
-                        lhsT=w1_codes[t][:].bitcast(FP8X4),
-                        lhsT_scale=w1_scales[t][:],
+                        lhsT=w1_codes[:, t * P : (t + 1) * P].bitcast(FP8X4),
+                        lhsT_scale=w1_scales[:, t * P : (t + 1) * P],
                         rhs=xw[d][:, v].bitcast(FP8X4),
                         rhs_scale=xs[d][:, v],
                         start=(n == 0),
@@ -125,18 +114,16 @@ def tile_picked_statpool_none_p_kernel(
         W = PACK * CHUNK
         st = [dict() for k in range(CHUNKS)]
 
-        def stage_a(k):
-            s = st[k]
+        def third_of(k, bank):
             third = work.tile([P, W], F32, name="third")
-            if k == 0:
-                h0 = first_product("h0", (0,), k)
-                nc.scalar.activation(woven(third), h0, ACT.Copy, scale=1.0 / 3.0)
-                s["other"] = first_product("h01", (1,), k)
-            else:
-                h01 = first_product("h01", (0, 1), k)
-                nc.scalar.activation(woven(third), h01, ACT.Copy, scale=1.0 / 3.0)
-                s["other"] = first_product("h0", (0,), k)
-            s["third"] = third
+            nc.scalar.activation(woven(third), bank, ACT.Copy, scale=1.0 / 3.0)
+            st[k]["third"] = third
+
+        def single(k):
+            st[k]["other"] = first_product("h0", (0,), k)
+
+        def paired(k):
+            third_of(k, first_product("h01", (0, 1), k))
 
         def halves(k):
             return (slice(0, CHUNK // 2), slice(CHUNK // 2, CHUNK)) if k in (3,) else (slice(0, CHUNK),)
@@ -196,7 +183,7 @@ def tile_picked_statpool_none_p_kernel(
             s = st[k]
             mean_q = quantize(s["mean"], "mean")
             dev_q = quantize(s["dev"], "dev")
-            acc = psum.tile([P, CHUNK], F32, name="acc")
+            acc = psum.tile([P, CHUNK], F32, name=("acc", "acc", "h0", "h01")[k])
             for n, (codes, (vals, scales)) in enumerate(((w2_codes, mean_q), (w3_codes, dev_q))):
                 nc.tensor.matmul_mx(
                     out=acc[:],
@@ -208,19 +195,23 @@ def tile_picked_statpool_none_p_kernel(
                     stop=(n == 1),
                 )
             res = work.tile([P, CHUNK], F32, name="res")
-            nc.scalar.copy(res[:], acc[:])
+            (nc.vector.tensor_copy if k == CHUNKS - 1 else nc.scalar.copy)(res[:], acc[:])
             nc.sync.dma_start(out[:, k * CHUNK : (k + 1) * CHUNK], res[:])
 
         last = CHUNKS - 1
-        stage_a(0)
+        third_of(0, first_product("h0", (0,), 0))
+        single(1)
+        st[0]["other"] = first_product("h01", (1,), 0)
+        paired(1)
         for k in range(CHUNKS):
-            if k < last:
-                stage_a(k + 1)
             differences(k)
-            if 0 < k:
-                mean_of(k - 1) if k == last else None
+            if k + 2 < CHUNKS:
+                paired(k + 2)
+                single(k + 2)
             if k < last - 1:
                 mean_of(k)
+            if k == last:
+                mean_of(k - 1)
             variance(k)
             if k > 0:
                 deviation(k - 1)

@@ -20,7 +20,6 @@ P = 128
 PACK = 4
 CHUNK = 128
 CHUNKS = V // CHUNK
-W1_PIECES = ()
 SQRT_FLOOR = 2.0**-116
 
 
@@ -37,7 +36,7 @@ def tile_picked_statpool_none_p_kernel(
         xs_table = keep.tile([P, T], U8, name="xs_table", tag="scale_rows", align_bytes=64)
         nc.vector.memset(xs_table[:].bitcast(I32), 0)
         warm_in = keep.tile([P, 1], F32, name="warm_in", tag="x_words", align_bytes=64)
-        warm_out = keep.tile([P, 1], F32, name="warm_out", tag="w1_late", align_bytes=64)
+        warm_out = keep.tile([P, 1], F32, name="warm_out")
         nc.gpsimd.memset(warm_in[:], 1.0)
         nc.scalar.activation(warm_out[:], warm_in[:], ACT.Sqrt)
 
@@ -47,21 +46,18 @@ def tile_picked_statpool_none_p_kernel(
             for r in range(4):
                 nc.sync.dma_start(tile_cols[r:P:32, :].bitcast(I32), rows[r:16:4, :].bitcast(I32))
 
-        w1_early = keep.tile([P, PACK, H // 2], F32, name="w1_early", tag="w1_early", align_bytes=64)
+        w1_raw = keep.tile([P, PACK, H], F32, name="w1_raw", tag="w1_early", align_bytes=64)
         nc.sync.dma_start(offsets[:], offs)
-        nc.sync.dma_start(w1_early[:], w1_rows[:, :, 0 : H // 2])
+        nc.sync.dma_start(w1_raw[:], w1_rows)
         load_scale_rows(xs_table[:], x_scales[0])
-        w1_late = keep.tile([P, PACK, H // 2], F32, name="w1_late", tag="w1_late", align_bytes=64)
         x_table = keep.tile([P, T], I32, name="x_table", tag="x_words", align_bytes=64)
-        nc.sync.dma_start(w1_late[:], w1_rows[:, :, H // 2 : H])
         nc.sync.dma_start(x_table[:], x_words[0].rearrange("p n t -> p (n t)").bitcast(I32))
 
         w1_bf = keep.tile([P, PACK, P, PACK], BF16, name="w1_bf", tag="w1_bf", align_bytes=64)
-        for half, raw in enumerate((w1_early, w1_late)):
-            nc.scalar.copy(
-                w1_bf[:, :, half * P // 2 : (half + 1) * P // 2, :].rearrange("p t m j -> p m t j"),
-                raw[:].rearrange("p j (m t) -> p m t j", t=PACK),
-            )
+        nc.scalar.copy(
+            w1_bf[:].rearrange("p t m j -> p m t j"),
+            w1_raw[:].rearrange("p j (m t) -> p m t j", t=PACK),
+        )
         w23_codes = keep.tile([P, 4 * N], U8, name="w23_codes", tag="w1_early", align_bytes=64)
         w2_codes = w23_codes[:, 0 : 2 * N]
         w3_codes = w23_codes[:, 2 * N : 4 * N]
@@ -74,21 +70,21 @@ def tile_picked_statpool_none_p_kernel(
         xw = [keep.tile([P, V], U32, name=f"xw{d}", align_bytes=64) for d in range(3)]
         nc.vector.tensor_copy(xs_all[:], xs_table[:].indirect(offsets[:]))
 
-        w23_scales = keep.tile([P, 2 * N], U8, name="w23_scales", tag="scale_rows", align_bytes=64)
-        nc.gpsimd.memset(w23_scales[:].bitcast(I32), 0)
-        load_scale_rows(w23_scales[:, 0:N], w2_scales[0])
-        load_scale_rows(w23_scales[:, N : 2 * N], w3_scales[0])
-
         def gather_words(d):
             nc.vector.tensor_copy(xw[d][:], x_table[:].bitcast(U32).indirect(offsets[:, d * cols : (d + 1) * cols]))
 
-        w1_codes = keep.tile([P, H], U32, name="w1_codes", align_bytes=64)
+        w1_codes = keep.tile([P, H], U32, name="w1_codes", tag="scale_rows", align_bytes=64)
         w1_scales = keep.tile([P, H], U8, name="w1_scales", align_bytes=64)
         nc.vector.quantize_mx(
             out=w1_codes[:].bitcast(FP8X4),
             scales=w1_scales[:],
             in_=w1_bf[:].rearrange("p t m j -> p (t m j)"),
         )
+        w23_scales = keep.tile([P, 2 * N], U8, name="w23_scales", tag="w1_bf", align_bytes=64)
+        nc.gpsimd.memset(w23_scales[:].bitcast(I32), 0)
+        load_scale_rows(w23_scales[:, 0:N], w2_scales[0])
+        load_scale_rows(w23_scales[:, N : 2 * N], w3_scales[0])
+
         for d in range(3):
             gather_words(d)
 
@@ -201,7 +197,7 @@ def tile_picked_statpool_none_p_kernel(
         last = CHUNKS - 1
         third_of(0, first_product("h0", (0,), 0))
         single(1)
-        st[0]["other"] = first_product("h01", (1,), 0)
+        st[0]["other"] = first_product("acc", (1,), 0)
         paired(1)
         for k in range(CHUNKS):
             differences(k)

@@ -35,10 +35,10 @@ def tile_picked_statpool_none_p_kernel(
         offsets = keep.tile([P, S // 16], U16, name="offsets")
         xs_table = keep.tile([P, T], U8, name="xs_table", tag="scale_rows", align_bytes=64)
         nc.vector.memset(xs_table[:].bitcast(I32), 0)
-        warm_in = keep.tile([P, 1], F32, name="warm_in", tag="x_words", align_bytes=64)
-        warm_out = keep.tile([P, 1], F32, name="warm_out")
-        nc.gpsimd.memset(warm_in[:], 1.0)
-        nc.scalar.activation(warm_out[:], warm_in[:], ACT.Sqrt)
+        one = keep.tile([P, 1], F32, name="one", tag="x_words", align_bytes=64)
+        root_third = keep.tile([P, 1], F32, name="root_third")
+        nc.gpsimd.memset(one[:], 1.0)
+        nc.scalar.activation(root_third[:], one[:], ACT.Sqrt, scale=1.0 / 3.0)
 
         w1_rows = w1.rearrange("(p j) c -> p j c", j=PACK)
 
@@ -49,7 +49,7 @@ def tile_picked_statpool_none_p_kernel(
         w1_raw = keep.tile([P, PACK, H], F32, name="w1_raw", tag="w1_early", align_bytes=64)
         nc.sync.dma_start(offsets[:], offs)
         nc.sync.dma_start(w1_raw[:], w1_rows)
-        load_scale_rows(xs_table[:], x_scales[0])
+        nc.sync.dma_start(xs_table[0:P:8, :].bitcast(I32), x_scales[0].bitcast(I32))
         x_table = keep.tile([P, T], I32, name="x_table", tag="x_words", align_bytes=64)
         nc.sync.dma_start(x_table[:], x_words[0].rearrange("p n t -> p (n t)").bitcast(I32))
 
@@ -68,7 +68,11 @@ def tile_picked_statpool_none_p_kernel(
         xs_all = keep.tile([P, S], U8, name="xs_all", align_bytes=64)
         xs = [xs_all[:, d * V : (d + 1) * V] for d in range(3)]
         xw = [keep.tile([P, V], U32, name=f"xw{d}", align_bytes=64) for d in range(3)]
-        nc.vector.tensor_copy(xs_all[:], xs_table[:].indirect(offsets[:]))
+        xs_picked = keep.tile([P, S], U8, name="xs_picked", align_bytes=64)
+        nc.gpsimd.memset(xs_all[:].bitcast(I32), 0)
+        nc.vector.tensor_copy(xs_picked[:], xs_table[:].indirect(offsets[:]))
+        for r in range(4):
+            nc.scalar.dma_start(xs_all[r:P:32, :].bitcast(I32), xs_picked[8 * r : P : 32, :].bitcast(I32))
 
         def gather_words(d):
             nc.vector.tensor_copy(xw[d][:], x_table[:].bitcast(U32).indirect(offsets[:, d * cols : (d + 1) * cols]))
@@ -150,14 +154,14 @@ def tile_picked_statpool_none_p_kernel(
             s = st[k]
             q2 = work.tile([P, W], F32, name="q2")
             r2 = work.tile([P, W], F32, name="r2")
-            var = work.tile([P, W], F32, name="var")
+            var = keep.tile([P, W], F32, name="last_var") if k == CHUNKS - 1 else work.tile([P, W], F32, name="var")
             if k in (0,):
                 nc.gpsimd.tensor_tensor(q2[:], s["q"][:], s["q"][:], ALU.mult)
             else:
                 nc.scalar.activation(q2[:], s["q"][:], ACT.Square)
             eng = nc.gpsimd if k in (0, 1, 2) else nc.vector
             for v in halves(k):
-                nc.scalar.activation(woven(r2)[:, v], woven(s["r"])[:, v], ACT.Square, scale=(1.0 / 3.0) ** 0.5)
+                nc.scalar.activation(woven(r2)[:, v], woven(s["r"])[:, v], ACT.Square, scale=root_third[:])
             for v in halves(k):
                 eng.tensor_tensor(woven(var)[:, v], woven(q2)[:, v], woven(r2)[:, v], ALU.add)
             s["var"] = var
@@ -175,24 +179,23 @@ def tile_picked_statpool_none_p_kernel(
             nc.vector.quantize_mx(out=codes[:].bitcast(FP8X4), scales=scales[:], in_=values[:])
             return codes, scales
 
-        def second_product(k):
-            s = st[k]
-            mean_q = quantize(s["mean"], "mean")
-            dev_q = quantize(s["dev"], "dev")
-            acc = psum.tile([P, CHUNK], F32, name=("acc", "acc", "h0", "h01")[k])
-            for n, (codes, (vals, scales)) in enumerate(((w2_codes, mean_q), (w3_codes, dev_q))):
-                nc.tensor.matmul_mx(
-                    out=acc[:],
-                    lhsT=codes.bitcast(FP4X4),
-                    lhsT_scale=w23_scales[:, n * N : (n + 1) * N],
-                    rhs=vals[:].bitcast(FP8X4),
-                    rhs_scale=scales[:],
-                    start=(n == 0),
-                    stop=(n == 1),
-                )
-            res = work.tile([P, CHUNK], F32, name="res")
-            (nc.vector.tensor_copy if k == CHUNKS - 1 else nc.scalar.copy)(res[:], acc[:])
-            nc.sync.dma_start(out[:, k * CHUNK : (k + 1) * CHUNK], res[:])
+        def second_product(chunks, name, copy, res):
+            acc = psum.tile([P, len(chunks) * CHUNK], F32, name=name)
+            for place, k in enumerate(chunks):
+                mean_q = quantize(st[k]["mean"], "mean")
+                dev_q = quantize(st[k]["dev"], "dev")
+                for n, (codes, (vals, scales)) in enumerate(((w2_codes, mean_q), (w3_codes, dev_q))):
+                    nc.tensor.matmul_mx(
+                        out=acc[:, place * CHUNK : (place + 1) * CHUNK],
+                        lhsT=codes.bitcast(FP4X4),
+                        lhsT_scale=w23_scales[:, n * N : (n + 1) * N],
+                        rhs=vals[:].bitcast(FP8X4),
+                        rhs_scale=scales[:],
+                        start=(n == 0),
+                        stop=(n == 1),
+                    )
+            copy(res[:], acc[:])
+            nc.sync.dma_start(out[:, chunks[0] * CHUNK : (chunks[-1] + 1) * CHUNK], res[:])
 
         last = CHUNKS - 1
         third_of(0, first_product("h0", (0,), 0))
@@ -213,5 +216,7 @@ def tile_picked_statpool_none_p_kernel(
                 deviation(k - 1)
         mean_of(last)
         deviation(last)
-        for k in range(CHUNKS):
-            second_product(k)
+        res_early = keep.tile([P, last * CHUNK], F32, name="res_early", tag="last_var")
+        second_product(range(last), "acc", nc.scalar.copy, res_early)
+        res_last = keep.tile([P, CHUNK], F32, name="res_last")
+        second_product((last,), "h01", nc.vector.tensor_copy, res_last)

@@ -1,6 +1,8 @@
+import math
 from contextlib import ExitStack
 
 import concourse.mybir as mybir
+from concourse.masks import make_identity
 
 K, T, S, V, H, N = 512, 4096, 1536, 512, 512, 128
 FLOPS = 2 * K * H * S + 2 * 2 * H * N * V
@@ -21,6 +23,9 @@ PACK = 4
 CHUNK = 128
 CHUNKS = V // CHUNK
 SQRT_FLOOR = 2.0**-116
+TURNED = (2, 3)
+HOLDS = {(2, "c0"): "means", (3, "c0"): "devs"}
+ACCTAG = "abab"
 
 
 def tile_picked_statpool_none_p_kernel(
@@ -36,33 +41,41 @@ def tile_picked_statpool_none_p_kernel(
         xs_table = keep.tile([P, T], U8, name="xs_table", tag="scale_rows", align_bytes=64)
         nc.vector.memset(xs_table[:].bitcast(I32), 0)
         one = keep.tile([P, 1], F32, name="one", tag="x_words", align_bytes=64)
-        root_third = keep.tile([P, 1], F32, name="root_third")
+        root_three = keep.tile([P, 1], F32, name="root_three")
         nc.gpsimd.memset(one[:], 1.0)
-        nc.scalar.activation(root_third[:], one[:], ACT.Sqrt, scale=1.0 / 3.0)
 
         w1_rows = w1.rearrange("(p j) c -> p j c", j=PACK)
-
-        def load_scale_rows(tile_cols, rows):
-            for r in range(4):
-                nc.sync.dma_start(tile_cols[r:P:32, :].bitcast(I32), rows[r:16:4, :].bitcast(I32))
-
-        w1_raw = keep.tile([P, PACK, H], F32, name="w1_raw", tag="w1_early", align_bytes=64)
+        w1_raw = [keep.tile([P, PACK, H // 2], F32, name=f"w1_raw{g}", align_bytes=64) for g in range(2)]
+        nc.sync.dma_start(w1_raw[0][:], w1_rows[:, :, : H // 2])
         nc.sync.dma_start(offsets[:], offs)
-        nc.sync.dma_start(w1_raw[:], w1_rows)
-        nc.sync.dma_start(xs_table[0:P:8, :].bitcast(I32), x_scales[0].bitcast(I32))
+        nc.sync.dma_start(w1_raw[1][:], w1_rows[:, :, H // 2 :])
+        nc.scalar.activation(root_three[:], one[:], ACT.Sqrt, scale=3.0)
+        nc.scalar.dma_start(xs_table[0:P:8, :].bitcast(I32), x_scales[0].bitcast(I32))
         x_table = keep.tile([P, T], I32, name="x_table", tag="x_words", align_bytes=64)
         nc.sync.dma_start(x_table[:], x_words[0].rearrange("p n t -> p (n t)").bitcast(I32))
 
         w1_bf = keep.tile([P, PACK, P, PACK], BF16, name="w1_bf", tag="w1_bf", align_bytes=64)
-        nc.scalar.copy(
-            w1_bf[:].rearrange("p t m j -> p m t j"),
-            w1_raw[:].rearrange("p j (m t) -> p m t j", t=PACK),
-        )
-        w23_codes = keep.tile([P, 4 * N], U8, name="w23_codes", tag="w1_early", align_bytes=64)
+        for g in range(2):
+            nc.scalar.copy(
+                w1_bf[:, :, g * P // 2 : (g + 1) * P // 2, :].rearrange("p t m j -> p m t j"),
+                w1_raw[g][:].rearrange("p j (m t) -> p m t j", t=PACK),
+            )
+        w1_minus = keep.tile([P, PACK, P, PACK], BF16, name="w1_minus", align_bytes=64)
+        for g in range(2):
+            nc.scalar.activation(
+                w1_minus[:, :, g * P // 2 : (g + 1) * P // 2, :].rearrange("p t m j -> p m t j"),
+                w1_raw[g][:].rearrange("p j (m t) -> p m t j", t=PACK),
+                ACT.Copy,
+                scale=-1.0,
+            )
+        w23_codes = keep.tile([P, 4 * N], U8, name="w23_codes", tag="w1_raw0", align_bytes=64)
         w2_codes = w23_codes[:, 0 : 2 * N]
         w3_codes = w23_codes[:, 2 * N : 4 * N]
         nc.sync.dma_start(w2_codes.bitcast(I32), w2_words[0].bitcast(I32))
         nc.sync.dma_start(w3_codes.bitcast(I32), w3_words[0].bitcast(I32))
+
+        identity = keep.tile([P, P], F32, name="identity")
+        make_identity(nc, identity[:])
 
         cols = V // 16
         xs_all = keep.tile([P, S], U8, name="xs_all", align_bytes=64)
@@ -72,151 +85,240 @@ def tile_picked_statpool_none_p_kernel(
         nc.gpsimd.memset(xs_all[:].bitcast(I32), 0)
         nc.vector.tensor_copy(xs_picked[:], xs_table[:].indirect(offsets[:]))
         for r in range(4):
-            nc.scalar.dma_start(xs_all[r:P:32, :].bitcast(I32), xs_picked[8 * r : P : 32, :].bitcast(I32))
+            nc.sync.dma_start(xs_all[r:P:32, :].bitcast(I32), xs_picked[8 * r : P : 32, :].bitcast(I32))
 
-        def gather_words(d):
-            nc.vector.tensor_copy(xw[d][:], x_table[:].bitcast(U32).indirect(offsets[:, d * cols : (d + 1) * cols]))
-
-        w1_codes = keep.tile([P, H], U32, name="w1_codes", tag="scale_rows", align_bytes=64)
-        w1_scales = keep.tile([P, H], U8, name="w1_scales", align_bytes=64)
-        nc.vector.quantize_mx(
-            out=w1_codes[:].bitcast(FP8X4),
-            scales=w1_scales[:],
-            in_=w1_bf[:].rearrange("p t m j -> p (t m j)"),
-        )
-        w23_scales = keep.tile([P, 2 * N], U8, name="w23_scales", tag="w1_bf", align_bytes=64)
+        w1_codes = keep.tile([P, 2 * H], U32, name="w1_codes", align_bytes=64)
+        w1_scales = keep.tile([P, 2 * H], U8, name="w1_scales", align_bytes=64)
+        for sign, values in enumerate((w1_bf, w1_minus)):
+            nc.vector.quantize_mx(
+                out=w1_codes[:, sign * H : (sign + 1) * H].bitcast(FP8X4),
+                scales=w1_scales[:, sign * H : (sign + 1) * H],
+                in_=values[:].rearrange("p t m j -> p (t m j)"),
+            )
+        w23_scales = keep.tile([P, 2 * N], U8, name="w23_scales", tag="xs_picked", align_bytes=64)
         nc.gpsimd.memset(w23_scales[:].bitcast(I32), 0)
-        load_scale_rows(w23_scales[:, 0:N], w2_scales[0])
-        load_scale_rows(w23_scales[:, N : 2 * N], w3_scales[0])
+        for n, rows in enumerate((w2_scales[0], w3_scales[0])):
+            for r in range(4):
+                nc.sync.dma_start(w23_scales[r:P:32, n * N : (n + 1) * N].bitcast(I32), rows[r:16:4, :].bitcast(I32))
 
         for d in range(3):
-            gather_words(d)
+            nc.vector.tensor_copy(xw[d][:], x_table[:].bitcast(U32).indirect(offsets[:, d * cols : (d + 1) * cols]))
+
+        W = PACK * CHUNK
+        last = CHUNKS - 1
+        st = [dict() for k in range(CHUNKS)]
+
+        def woven(tile):
+            return tile[:].rearrange("p (v t) -> p v t", t=PACK)
 
         def first_product(tag, pieces, k):
-            bank = psum.tile([P, PACK, CHUNK], F32, name=tag)
             v = slice(k * CHUNK, (k + 1) * CHUNK)
-            for t in range(PACK):
-                for n, d in enumerate(pieces):
+            bank = psum.tile([P, H], F32, name=tag, bufs=CHUNKS)
+            if k in TURNED:
+                for n, (d, sign) in enumerate(pieces):
+                    m = slice(sign * H, (sign + 1) * H)
                     nc.tensor.matmul_mx(
-                        out=bank[:, t, :],
-                        lhsT=w1_codes[:, t * P : (t + 1) * P].bitcast(FP8X4),
-                        lhsT_scale=w1_scales[:, t * P : (t + 1) * P],
+                        out=bank[:],
+                        lhsT=xw[d][:, v].bitcast(FP8X4),
+                        lhsT_scale=xs[d][:, v],
+                        rhs=w1_codes[:, m].bitcast(FP8X4),
+                        rhs_scale=w1_scales[:, m],
+                        start=(n == 0),
+                        stop=(n == len(pieces) - 1),
+                    )
+                return bank[:]
+            for t in range(PACK):
+                for n, (d, sign) in enumerate(pieces):
+                    m = slice(sign * H + t * P, sign * H + (t + 1) * P)
+                    nc.tensor.matmul_mx(
+                        out=bank[:, t * CHUNK : (t + 1) * CHUNK],
+                        lhsT=w1_codes[:, m].bitcast(FP8X4),
+                        lhsT_scale=w1_scales[:, m],
                         rhs=xw[d][:, v].bitcast(FP8X4),
                         rhs_scale=xs[d][:, v],
                         start=(n == 0),
                         stop=(n == len(pieces) - 1),
                     )
-            return bank[:].rearrange("p t v -> p v t")
+            return bank[:].rearrange("p (t v) -> p v t", t=PACK)
 
-        def woven(tile):
-            return tile[:].rearrange("p (v t) -> p v t", t=PACK)
+        def laid(k, tile):
+            return tile[:] if k in TURNED else woven(tile)
 
-        W = PACK * CHUNK
-        st = [dict() for k in range(CHUNKS)]
+        def temp(k, name):
+            if (k, name) in HOLDS:
+                return keep.tile([P, W], F32, name=f"late_{name}", tag=HOLDS[(k, name)], align_bytes=64)
+            return work.tile([P, W], F32, name=name)
 
-        def third_of(k, bank):
-            third = work.tile([P, W], F32, name="third")
-            nc.scalar.activation(woven(third), bank, ACT.Copy, scale=1.0 / 3.0)
-            st[k]["third"] = third
-
-        def single(k):
-            st[k]["other"] = first_product("h0", (0,), k)
-
-        def paired(k):
-            third_of(k, first_product("h01", (0, 1), k))
-
-        def halves(k):
-            return (slice(0, CHUNK // 2), slice(CHUNK // 2, CHUNK)) if k in (3,) else (slice(0, CHUNK),)
-
-        def differences(k):
+        def copy_h0(k):
             s = st[k]
-            q = work.tile([P, W], F32, name="q")
-            r = work.tile([P, W], F32, name="r")
+            s["c0"] = temp(k, "c0")
+            nc.scalar.activation(laid(k, s["c0"]), first_product("a", ((0, 0),), k), ACT.Copy, scale=3.0 if k in TURNED else 2.0)
+
+        def second(k):
+            st[k]["u_bank"] = first_product("b", ((1, 0),) if k == 0 else ((1, 0), (0, 1)), k)
+
+        def third(k):
+            st[k]["h2"] = first_product("a", ((2, 0),), k)
+
+        def pair_of(k):
+            s = st[k]
+            s["pair"] = temp(k, "pair")
             if k == 0:
-                pair = work.tile([P, W], F32, name="pair")
-                nc.vector.scalar_tensor_tensor(woven(pair), s["other"], 1.0 / 3.0, woven(s["third"]), ALU.mult, ALU.add)
-                nc.vector.scalar_tensor_tensor(woven(q), s["other"], 1.0 / 3.0, woven(s["third"]), ALU.mult, ALU.subtract)
+                nc.vector.scalar_tensor_tensor(woven(s["pair"]), woven(s["c0"]), 0.5, s["u_bank"], ALU.mult, ALU.add)
             else:
-                pair = s["third"]
-                nc.vector.scalar_tensor_tensor(woven(q), s["other"], 2.0 / 3.0, woven(pair), ALU.mult, ALU.subtract)
-            h2 = first_product("h2", (2,), k)
-            for v in halves(k):
-                nc.vector.scalar_tensor_tensor(woven(r)[:, v], h2[:, v], 2.0 / 3.0, woven(pair)[:, v], ALU.mult, ALU.subtract)
-            s["q"], s["r"], s["h2"], s["pair"] = q, r, h2, pair
+                nc.vector.scalar_tensor_tensor(
+                    laid(k, s["pair"]), s["u_bank"], 1.5 if k in TURNED else 1.0, laid(k, s["c0"]), ALU.mult, ALU.add
+                )
 
-        def mean_of(k):
-            s = st[k]
-            mean = work.tile([P, W], BF16, name="mean", align_bytes=64)
-            nc.vector.scalar_tensor_tensor(woven(mean), s["h2"], 1.0 / 3.0, woven(s["pair"]), ALU.mult, ALU.add)
-            s["mean"] = mean
+        def u_of_first():
+            s = st[0]
+            u = temp(0, "u")
+            nc.vector.scalar_tensor_tensor(woven(u), woven(s["c0"]), -0.5, s["u_bank"], ALU.mult, ALU.add)
+            s["u_bank"] = woven(u)
 
-        def variance(k):
+        def diff_r(k):
             s = st[k]
-            q2 = work.tile([P, W], F32, name="q2")
-            r2 = work.tile([P, W], F32, name="r2")
-            var = keep.tile([P, W], F32, name="last_var") if k == CHUNKS - 1 else work.tile([P, W], F32, name="var")
-            if k in (0,):
-                nc.gpsimd.tensor_tensor(q2[:], s["q"][:], s["q"][:], ALU.mult)
+            s["r"] = temp(k, "r")
+            if k in TURNED:
+                nc.vector.scalar_tensor_tensor(s["r"][:], s["pair"][:], -1.0 / 3.0, s["h2"], ALU.mult, ALU.add)
             else:
-                nc.scalar.activation(q2[:], s["q"][:], ACT.Square)
-            eng = nc.gpsimd if k in (0, 1, 2) else nc.vector
-            for v in halves(k):
-                nc.scalar.activation(woven(r2)[:, v], woven(s["r"])[:, v], ACT.Square, scale=root_third[:])
-            for v in halves(k):
-                eng.tensor_tensor(woven(var)[:, v], woven(q2)[:, v], woven(r2)[:, v], ALU.add)
-            s["var"] = var
+                nc.vector.scalar_tensor_tensor(woven(s["r"]), s["h2"], 2.0, woven(s["pair"]), ALU.mult, ALU.subtract)
 
-        def deviation(k):
+        def square_u(k):
             s = st[k]
-            dev = work.tile([P, W], BF16, name="dev", align_bytes=64)
-            for v in halves(k):
-                nc.scalar.activation(woven(dev)[:, v], woven(s["var"])[:, v], ACT.Sqrt, scale=1.5, bias=SQRT_FLOOR)
-            s["dev"] = dev
+            s["u2"] = temp(k, "u2")
+            scale = math.sqrt(0.75) if k in TURNED else root_three[:]
+            nc.scalar.activation(laid(k, s["u2"]), s["u_bank"], ACT.Square, scale=scale)
 
-        def quantize(values, name):
-            codes = work.tile([P, CHUNK], U32, name=name + "_codes", align_bytes=64)
-            scales = work.tile([P, CHUNK], U8, name=name + "_scales", align_bytes=64)
-            nc.vector.quantize_mx(out=codes[:].bitcast(FP8X4), scales=scales[:], in_=values[:])
-            return codes, scales
+        def square_r(k, on_gpsimd):
+            s = st[k]
+            s["r2"] = temp(k, "r2")
+            if on_gpsimd:
+                nc.gpsimd.tensor_tensor(s["r2"][:], s["r"][:], s["r"][:], ALU.mult)
+            else:
+                nc.scalar.activation(s["r2"][:], s["r"][:], ACT.Square)
 
-        def second_product(chunks, name, copy, res):
-            acc = psum.tile([P, len(chunks) * CHUNK], F32, name=name)
+        def variance(k, eng):
+            s = st[k]
+            s["var"] = temp(k, "var")
+            eng.tensor_tensor(s["var"][:], s["u2"][:], s["r2"][:], ALU.add)
+
+        def turn(k, target, tag, name, first):
+            s = st[k]
+            if first:
+                s[target] = psum.tile([P, PACK, CHUNK], F32, name=tag, bufs=CHUNKS)
+            for t in range(PACK):
+                nc.tensor.matmul(
+                    s[target][:, t, :],
+                    s[name][:, t * P : (t + 1) * P],
+                    identity[:],
+                    is_transpose=True,
+                    start=first and t == 0,
+                    stop=not first and t == PACK - 1,
+                )
+
+        def mean_of(k, means, on_scalar=False):
+            s = st[k]
+            target = woven(means[:, k * W : (k + 1) * W])
+            if k not in TURNED:
+                nc.vector.scalar_tensor_tensor(target, woven(s["r"]), -1.0 / 3.0, s["h2"], ALU.mult, ALU.add)
+            elif on_scalar:
+                nc.scalar.activation(target, s["sum"][:].rearrange("p t v -> p v t"), ACT.Copy, scale=1.0 / 3.0)
+            else:
+                nc.vector.tensor_scalar(target, s["sum"][:].rearrange("p t v -> p v t"), 1.0 / 3.0, None, ALU.mult)
+
+        def deviation(k, devs):
+            target = devs[:, k * W : (k + 1) * W]
+            if k in TURNED:
+                nc.scalar.activation(woven(target), st[k]["var"][:].rearrange("p t v -> p v t"), ACT.Sqrt, scale=2.0 / 9.0, bias=SQRT_FLOOR)
+            else:
+                nc.scalar.activation(target, st[k]["var"][:], ACT.Sqrt, scale=1.0 / 18.0, bias=SQRT_FLOOR)
+
+        mean_codes = keep.tile([P, V], U32, name="mean_codes", align_bytes=64)
+        mean_scales = keep.tile([P, V], U8, name="mean_scales", align_bytes=64)
+        dev_codes = keep.tile([P, V], U32, name="dev_codes", align_bytes=64)
+        dev_scales = keep.tile([P, V], U8, name="dev_scales", align_bytes=64)
+
+        def quantize(values, codes, scales, first, count):
+            v = slice(first * CHUNK, (first + count) * CHUNK)
+            nc.vector.quantize_mx(out=codes[:, v].bitcast(FP8X4), scales=scales[:, v], in_=values[:, first * W : (first + count) * W])
+
+        def second_pass(k, n):
+            v = slice(k * CHUNK, (k + 1) * CHUNK)
+            if n == 0:
+                st[k]["acc"] = psum.tile([P, CHUNK], F32, name=ACCTAG[k], bufs=CHUNKS)
+            codes, vals, scales = ((w2_codes, mean_codes, mean_scales), (w3_codes, dev_codes, dev_scales))[n]
+            nc.tensor.matmul_mx(
+                out=st[k]["acc"][:],
+                lhsT=codes.bitcast(FP4X4),
+                lhsT_scale=w23_scales[:, n * N : (n + 1) * N],
+                rhs=vals[:, v].bitcast(FP8X4),
+                rhs_scale=scales[:, v],
+                start=(n == 0),
+                stop=(n == 1),
+            )
+
+        def store(chunks, copy):
+            res = work.tile([P, len(chunks) * CHUNK], F32, name="res")
             for place, k in enumerate(chunks):
-                mean_q = quantize(st[k]["mean"], "mean")
-                dev_q = quantize(st[k]["dev"], "dev")
-                for n, (codes, (vals, scales)) in enumerate(((w2_codes, mean_q), (w3_codes, dev_q))):
-                    nc.tensor.matmul_mx(
-                        out=acc[:, place * CHUNK : (place + 1) * CHUNK],
-                        lhsT=codes.bitcast(FP4X4),
-                        lhsT_scale=w23_scales[:, n * N : (n + 1) * N],
-                        rhs=vals[:].bitcast(FP8X4),
-                        rhs_scale=scales[:],
-                        start=(n == 0),
-                        stop=(n == 1),
-                    )
-            copy(res[:], acc[:])
+                copy(res[:, place * CHUNK : (place + 1) * CHUNK], st[k]["acc"][:])
             nc.sync.dma_start(out[:, chunks[0] * CHUNK : (chunks[-1] + 1) * CHUNK], res[:])
 
-        last = CHUNKS - 1
-        third_of(0, first_product("h0", (0,), 0))
-        single(1)
-        st[0]["other"] = first_product("acc", (1,), 0)
-        paired(1)
-        for k in range(CHUNKS):
-            differences(k)
-            if k + 2 < CHUNKS:
-                paired(k + 2)
-                single(k + 2)
-            if k < last - 1:
-                mean_of(k)
-            if k == last:
-                mean_of(k - 1)
-            variance(k)
-            if k > 0:
-                deviation(k - 1)
-        mean_of(last)
-        deviation(last)
-        res_early = keep.tile([P, last * CHUNK], F32, name="res_early", tag="last_var")
-        second_product(range(last), "acc", nc.scalar.copy, res_early)
-        res_last = keep.tile([P, CHUNK], F32, name="res_last")
-        second_product((last,), "h01", nc.vector.tensor_copy, res_last)
+        copy_h0(0)
+        copy_h0(1)
+        second(0)
+        second(1)
+        square_u(1)
+        third(0)
+        copy_h0(2)
+        third(1)
+        second(2)
+        copy_h0(3)
+        third(2)
+        second(3)
+        pair_of(0)
+        u_of_first()
+        diff_r(0)
+        pair_of(1)
+        square_u(0)
+        square_r(0, True)
+        variance(0, nc.gpsimd)
+        pair_of(2)
+        diff_r(1)
+        third(3)
+        square_r(1, False)
+        square_u(2)
+        diff_r(2)
+        variance(1, nc.gpsimd)
+        pair_of(3)
+        square_r(2, False)
+        square_u(3)
+        diff_r(3)
+        square_r(3, False)
+        for k in (2, 3):
+            turn(k, "sum", "b", "pair", True)
+            turn(k, "sum", "b", "r", False)
+            turn(k, "var", "a", "u2", True)
+            turn(k, "var", "a", "r2", False)
+        means = keep.tile([P, CHUNKS * W], BF16, name="means", tag="means", align_bytes=64)
+        devs = keep.tile([P, CHUNKS * W], BF16, name="devs", tag="devs", align_bytes=64)
+        mean_of(0, means)
+        mean_of(1, means)
+        mean_of(2, means)
+        quantize(means, mean_codes, mean_scales, 0, 2)
+        mean_of(3, means)
+        for k in (0, 1, 2, 3):
+            deviation(k, devs)
+        second_pass(0, 0)
+        second_pass(1, 0)
+        quantize(devs, dev_codes, dev_scales, 0, 2)
+        second_pass(0, 1)
+        second_pass(1, 1)
+        quantize(means, mean_codes, mean_scales, 2, 2)
+        second_pass(2, 0)
+        second_pass(3, 0)
+        for k in (2, 3):
+            quantize(devs, dev_codes, dev_scales, k, 1)
+            second_pass(k, 1)
+        store((0, 1), nc.scalar.copy)
+        store((2, 3), nc.vector.tensor_copy)

@@ -22,9 +22,11 @@ P = 128
 PACK = 4
 CHUNK = 128
 CHUNKS = V // CHUNK
+HALVED = ()
+CUTS = (0, 64, 112, 128)
 SQRT_FLOOR = 2.0**-116
-TURNED = (2, 3)
-HOLDS = {(2, "c0"): "means", (3, "c0"): "devs"}
+TURNED = (3,)
+HOLDS = {(2, "pair"): "means", (3, "c0"): "devs"}
 ACCTAG = "abab"
 
 
@@ -40,30 +42,41 @@ def tile_picked_statpool_none_p_kernel(
         offsets = keep.tile([P, S // 16], U16, name="offsets")
         xs_table = keep.tile([P, T], U8, name="xs_table", tag="scale_rows", align_bytes=64)
         nc.vector.memset(xs_table[:].bitcast(I32), 0)
-        one = keep.tile([P, 1], F32, name="one", tag="x_words", align_bytes=64)
+        one = keep.tile([P, 1], F32, name="one", tag="w1_raw2", align_bytes=64)
+        unit = keep.tile([P, 1], F32, name="unit", tag="x_words", align_bytes=64)
         root_three = keep.tile([P, 1], F32, name="root_three")
+        floor = keep.tile([P, 1], F32, name="floor")
         nc.gpsimd.memset(one[:], 1.0)
+        nc.gpsimd.memset(unit[:], 1.0)
 
         w1_rows = w1.rearrange("(p j) c -> p j c", j=PACK)
-        w1_raw = [keep.tile([P, PACK, H // 2], F32, name=f"w1_raw{g}", align_bytes=64) for g in range(2)]
-        nc.sync.dma_start(w1_raw[0][:], w1_rows[:, :, : H // 2])
+        w1_raw = []
+
+        def load_w1(g):
+            raw = keep.tile([P, PACK, PACK * (CUTS[g + 1] - CUTS[g])], F32, name=f"w1_raw{g}", align_bytes=64)
+            nc.sync.dma_start(raw[:], w1_rows[:, :, PACK * CUTS[g] : PACK * CUTS[g + 1]])
+            w1_raw.append(raw)
+
+        load_w1(0)
         nc.sync.dma_start(offsets[:], offs)
-        nc.sync.dma_start(w1_raw[1][:], w1_rows[:, :, H // 2 :])
+        load_w1(1)
         nc.scalar.activation(root_three[:], one[:], ACT.Sqrt, scale=3.0)
+        nc.scalar.activation(floor[:], unit[:], ACT.Copy, scale=SQRT_FLOOR)
         nc.scalar.dma_start(xs_table[0:P:8, :].bitcast(I32), x_scales[0].bitcast(I32))
+        load_w1(2)
         x_table = keep.tile([P, T], I32, name="x_table", tag="x_words", align_bytes=64)
         nc.sync.dma_start(x_table[:], x_words[0].rearrange("p n t -> p (n t)").bitcast(I32))
 
         w1_bf = keep.tile([P, PACK, P, PACK], BF16, name="w1_bf", tag="w1_bf", align_bytes=64)
-        for g in range(2):
+        for g in range(3):
             nc.scalar.copy(
-                w1_bf[:, :, g * P // 2 : (g + 1) * P // 2, :].rearrange("p t m j -> p m t j"),
+                w1_bf[:, :, CUTS[g] : CUTS[g + 1], :].rearrange("p t m j -> p m t j"),
                 w1_raw[g][:].rearrange("p j (m t) -> p m t j", t=PACK),
             )
         w1_minus = keep.tile([P, PACK, P, PACK], BF16, name="w1_minus", align_bytes=64)
-        for g in range(2):
+        for g in range(3):
             nc.scalar.activation(
-                w1_minus[:, :, g * P // 2 : (g + 1) * P // 2, :].rearrange("p t m j -> p m t j"),
+                w1_minus[:, :, CUTS[g] : CUTS[g + 1], :].rearrange("p t m j -> p m t j"),
                 w1_raw[g][:].rearrange("p j (m t) -> p m t j", t=PACK),
                 ACT.Copy,
                 scale=-1.0,
@@ -141,6 +154,9 @@ def tile_picked_statpool_none_p_kernel(
                     )
             return bank[:].rearrange("p (t v) -> p v t", t=PACK)
 
+        def halves(k):
+            return (slice(0, W // 2), slice(W // 2, W)) if k in HALVED else (slice(0, W),)
+
         def laid(k, tile):
             return tile[:] if k in TURNED else woven(tile)
 
@@ -196,12 +212,14 @@ def tile_picked_statpool_none_p_kernel(
             if on_gpsimd:
                 nc.gpsimd.tensor_tensor(s["r2"][:], s["r"][:], s["r"][:], ALU.mult)
             else:
-                nc.scalar.activation(s["r2"][:], s["r"][:], ACT.Square)
+                for v in halves(k):
+                    nc.scalar.activation(s["r2"][:, v], s["r"][:, v], ACT.Square)
 
         def variance(k, eng):
             s = st[k]
             s["var"] = temp(k, "var")
-            eng.tensor_tensor(s["var"][:], s["u2"][:], s["r2"][:], ALU.add)
+            for v in halves(k):
+                eng.tensor_tensor(s["var"][:, v], s["u2"][:, v], s["r2"][:, v], ALU.add)
 
         def turn(k, target, tag, name, first):
             s = st[k]
@@ -230,9 +248,10 @@ def tile_picked_statpool_none_p_kernel(
         def deviation(k, devs):
             target = devs[:, k * W : (k + 1) * W]
             if k in TURNED:
-                nc.scalar.activation(woven(target), st[k]["var"][:].rearrange("p t v -> p v t"), ACT.Sqrt, scale=2.0 / 9.0, bias=SQRT_FLOOR)
+                nc.scalar.activation(woven(target), st[k]["var"][:].rearrange("p t v -> p v t"), ACT.Sqrt, scale=2.0 / 9.0, bias=floor[:])
             else:
-                nc.scalar.activation(target, st[k]["var"][:], ACT.Sqrt, scale=1.0 / 18.0, bias=SQRT_FLOOR)
+                for v in halves(k):
+                    nc.scalar.activation(target[:, v], st[k]["var"][:, v], ACT.Sqrt, scale=1.0 / 18.0, bias=floor[:])
 
         mean_codes = keep.tile([P, V], U32, name="mean_codes", align_bytes=64)
         mean_scales = keep.tile([P, V], U8, name="mean_scales", align_bytes=64)
@@ -288,27 +307,29 @@ def tile_picked_statpool_none_p_kernel(
         third(3)
         square_r(1, False)
         square_u(2)
+        pair_of(3)
         diff_r(2)
         variance(1, nc.gpsimd)
-        pair_of(3)
         square_r(2, False)
+        variance(2, nc.gpsimd)
         square_u(3)
         diff_r(3)
         square_r(3, False)
-        for k in (2, 3):
-            turn(k, "sum", "b", "pair", True)
-            turn(k, "sum", "b", "r", False)
-            turn(k, "var", "a", "u2", True)
-            turn(k, "var", "a", "r2", False)
+        turn(3, "sum", "b", "pair", True)
+        turn(3, "var", "a", "u2", True)
+        turn(3, "sum", "b", "r", False)
+        turn(3, "var", "a", "r2", False)
         means = keep.tile([P, CHUNKS * W], BF16, name="means", tag="means", align_bytes=64)
         devs = keep.tile([P, CHUNKS * W], BF16, name="devs", tag="devs", align_bytes=64)
         mean_of(0, means)
         mean_of(1, means)
         mean_of(2, means)
-        quantize(means, mean_codes, mean_scales, 0, 2)
         mean_of(3, means)
-        for k in (0, 1, 2, 3):
-            deviation(k, devs)
+        quantize(means, mean_codes, mean_scales, 0, 2)
+        deviation(0, devs)
+        deviation(1, devs)
+        deviation(3, devs)
+        deviation(2, devs)
         second_pass(0, 0)
         second_pass(1, 0)
         quantize(devs, dev_codes, dev_scales, 0, 2)
@@ -317,7 +338,7 @@ def tile_picked_statpool_none_p_kernel(
         quantize(means, mean_codes, mean_scales, 2, 2)
         second_pass(2, 0)
         second_pass(3, 0)
-        for k in (2, 3):
+        for k in (3, 2):
             quantize(devs, dev_codes, dev_scales, k, 1)
             second_pass(k, 1)
         store((0, 1), nc.scalar.copy)

@@ -23,7 +23,7 @@ PACK = 4
 CHUNK = 128
 CHUNKS = V // CHUNK
 HALVED = ()
-CUTS = (0, 64, 112, 128)
+CUTS = (0, 80, 128)
 SQRT_FLOOR = 2.0**-116
 TURNED = (3,)
 HOLDS = {(2, "pair"): "means", (3, "c0"): "devs"}
@@ -41,13 +41,17 @@ def tile_picked_statpool_none_p_kernel(
 
         offsets = keep.tile([P, S // 16], U16, name="offsets")
         xs_table = keep.tile([P, T], U8, name="xs_table", tag="scale_rows", align_bytes=64)
-        nc.vector.memset(xs_table[:].bitcast(I32), 0)
-        one = keep.tile([P, 1], F32, name="one", tag="w1_raw2", align_bytes=64)
+        nc.gpsimd.memset(xs_table[:, : T // 2].bitcast(I32), 0)
+        nc.vector.memset(xs_table[:, T // 2 :].bitcast(I32), 0)
+        one = keep.tile([P, 1], F32, name="one", tag="w1_raw1", align_bytes=64)
         unit = keep.tile([P, 1], F32, name="unit", tag="x_words", align_bytes=64)
         root_three = keep.tile([P, 1], F32, name="root_three")
         floor = keep.tile([P, 1], F32, name="floor")
         nc.gpsimd.memset(one[:], 1.0)
         nc.gpsimd.memset(unit[:], 1.0)
+        three = keep.tile([P, 1], F32, name="three")
+        nc.vector.tensor_scalar(three[:], one[:], 3.0, None, ALU.mult)
+        nc.vector.tensor_scalar(floor[:], unit[:], SQRT_FLOOR, None, ALU.mult)
 
         w1_rows = w1.rearrange("(p j) c -> p j c", j=PACK)
         w1_raw = []
@@ -59,28 +63,21 @@ def tile_picked_statpool_none_p_kernel(
 
         load_w1(0)
         nc.sync.dma_start(offsets[:], offs)
-        load_w1(1)
-        nc.scalar.activation(root_three[:], one[:], ACT.Sqrt, scale=3.0)
-        nc.scalar.activation(floor[:], unit[:], ACT.Copy, scale=SQRT_FLOOR)
         nc.scalar.dma_start(xs_table[0:P:8, :].bitcast(I32), x_scales[0].bitcast(I32))
-        load_w1(2)
+        nc.scalar.activation(root_three[:], three[:], ACT.Sqrt)
+        load_w1(1)
         x_table = keep.tile([P, T], I32, name="x_table", tag="x_words", align_bytes=64)
         nc.sync.dma_start(x_table[:], x_words[0].rearrange("p n t -> p (n t)").bitcast(I32))
 
         w1_bf = keep.tile([P, PACK, P, PACK], BF16, name="w1_bf", tag="w1_bf", align_bytes=64)
-        for g in range(3):
+        for g in range(2):
             nc.scalar.copy(
                 w1_bf[:, :, CUTS[g] : CUTS[g + 1], :].rearrange("p t m j -> p m t j"),
                 w1_raw[g][:].rearrange("p j (m t) -> p m t j", t=PACK),
             )
-        w1_minus = keep.tile([P, PACK, P, PACK], BF16, name="w1_minus", align_bytes=64)
-        for g in range(3):
-            nc.scalar.activation(
-                w1_minus[:, :, CUTS[g] : CUTS[g + 1], :].rearrange("p t m j -> p m t j"),
-                w1_raw[g][:].rearrange("p j (m t) -> p m t j", t=PACK),
-                ACT.Copy,
-                scale=-1.0,
-            )
+        w1_flat = w1_bf[:].rearrange("p t m j -> p (t m j)")
+        w1_minus = keep.tile([P, PACK * H], BF16, name="w1_minus", align_bytes=64)
+        nc.scalar.activation(w1_minus[:, : 2 * H], w1_flat[:, : 2 * H], ACT.Copy, scale=-1.0)
         w23_codes = keep.tile([P, 4 * N], U8, name="w23_codes", tag="w1_raw0", align_bytes=64)
         w2_codes = w23_codes[:, 0 : 2 * N]
         w3_codes = w23_codes[:, 2 * N : 4 * N]
@@ -100,15 +97,16 @@ def tile_picked_statpool_none_p_kernel(
         for r in range(4):
             nc.sync.dma_start(xs_all[r:P:32, :].bitcast(I32), xs_picked[8 * r : P : 32, :].bitcast(I32))
 
+        nc.vector.tensor_scalar(w1_minus[:, 2 * H :], w1_flat[:, 2 * H :], -1.0, None, ALU.mult)
         w1_codes = keep.tile([P, 2 * H], U32, name="w1_codes", align_bytes=64)
         w1_scales = keep.tile([P, 2 * H], U8, name="w1_scales", align_bytes=64)
-        for sign, values in enumerate((w1_bf, w1_minus)):
+        for sign, values in enumerate((w1_flat, w1_minus[:])):
             nc.vector.quantize_mx(
                 out=w1_codes[:, sign * H : (sign + 1) * H].bitcast(FP8X4),
                 scales=w1_scales[:, sign * H : (sign + 1) * H],
-                in_=values[:].rearrange("p t m j -> p (t m j)"),
+                in_=values,
             )
-        w23_scales = keep.tile([P, 2 * N], U8, name="w23_scales", tag="xs_picked", align_bytes=64)
+        w23_scales = keep.tile([P, 2 * N], U8, name="w23_scales", tag="w1_minus", align_bytes=64)
         nc.gpsimd.memset(w23_scales[:].bitcast(I32), 0)
         for n, rows in enumerate((w2_scales[0], w3_scales[0])):
             for r in range(4):
@@ -342,4 +340,5 @@ def tile_picked_statpool_none_p_kernel(
             quantize(devs, dev_codes, dev_scales, k, 1)
             second_pass(k, 1)
         store((0, 1), nc.scalar.copy)
-        store((2, 3), nc.vector.tensor_copy)
+        store((3,), nc.vector.tensor_copy)
+        store((2,), nc.vector.tensor_copy)

@@ -22,8 +22,10 @@ P = 128
 PACK = 4
 CHUNK = 128
 CHUNKS = V // CHUNK
-HALVED = ()
+HALVED = (2, 3)
 CUTS = (0, 80, 128)
+HALF = H // 2
+SHARE = 256
 SQRT_FLOOR = 2.0**-116
 TURNED = (3,)
 HOLDS = {(2, "pair"): "means", (3, "c0"): "devs"}
@@ -106,8 +108,8 @@ def tile_picked_statpool_none_p_kernel(
                 scales=w1_scales[:, sign * H : (sign + 1) * H],
                 in_=values,
             )
-        w23_scales = keep.tile([P, 2 * N], U8, name="w23_scales", tag="w1_minus", align_bytes=64)
-        nc.gpsimd.memset(w23_scales[:].bitcast(I32), 0)
+        w23_scales = keep.tile([P, 2 * N], U8, name="w23_scales", tag="w1_bf", align_bytes=64)
+        nc.vector.memset(w23_scales[:].bitcast(I32), 0)
         for n, rows in enumerate((w2_scales[0], w3_scales[0])):
             for r in range(4):
                 nc.sync.dma_start(w23_scales[r:P:32, n * N : (n + 1) * N].bitcast(I32), rows[r:16:4, :].bitcast(I32))
@@ -153,7 +155,8 @@ def tile_picked_statpool_none_p_kernel(
             return bank[:].rearrange("p (t v) -> p v t", t=PACK)
 
         def halves(k):
-            return (slice(0, W // 2), slice(W // 2, W)) if k in HALVED else (slice(0, W),)
+            cut = W // 2 if k in TURNED else SHARE
+            return (slice(0, cut), slice(cut, W)) if k in HALVED else (slice(0, W),)
 
         def laid(k, tile):
             return tile[:] if k in TURNED else woven(tile)
@@ -167,6 +170,30 @@ def tile_picked_statpool_none_p_kernel(
             s = st[k]
             s["c0"] = temp(k, "c0")
             nc.scalar.activation(laid(k, s["c0"]), first_product("a", ((0, 0),), k), ACT.Copy, scale=3.0 if k in TURNED else 2.0)
+
+        def copy_turned(k):
+            s = st[k]
+            v = slice(k * CHUNK, (k + 1) * CHUNK)
+            bank = psum.tile([P, H], F32, name="a", bufs=CHUNKS)
+            for m, pieces in ((slice(0, HALF), (0, 1)), (slice(HALF, H), (0,))):
+                for n, d in enumerate(pieces):
+                    nc.tensor.matmul_mx(
+                        out=bank[:, m],
+                        lhsT=xw[d][:, v].bitcast(FP8X4),
+                        lhsT_scale=xs[d][:, v],
+                        rhs=w1_codes[:, m].bitcast(FP8X4),
+                        rhs_scale=w1_scales[:, m],
+                        start=(n == 0),
+                        stop=(n == len(pieces) - 1),
+                    )
+            s["c0"] = temp(k, "c0")
+            s["pair"] = keep.tile([P, W], F32, name="pair_turned")
+            nc.scalar.activation(s["c0"][:, HALF:], bank[:, HALF:], ACT.Copy, scale=3.0)
+            nc.scalar.activation(s["pair"][:, :HALF], bank[:, :HALF], ACT.Copy, scale=1.5)
+
+        def pair_turned(k):
+            s = st[k]
+            nc.vector.scalar_tensor_tensor(s["pair"][:, HALF:], s["u_bank"][:, HALF:], 1.5, s["c0"][:, HALF:], ALU.mult, ALU.add)
 
         def second(k):
             st[k]["u_bank"] = first_product("b", ((1, 0),) if k == 0 else ((1, 0), (0, 1)), k)
@@ -208,16 +235,22 @@ def tile_picked_statpool_none_p_kernel(
             s = st[k]
             s["r2"] = temp(k, "r2")
             if on_gpsimd:
-                nc.gpsimd.tensor_tensor(s["r2"][:], s["r"][:], s["r"][:], ALU.mult)
+                nc.gpsimd.tensor_tensor(s["r2"][:, :HALF], s["r"][:, :HALF], s["r"][:, :HALF], ALU.mult)
+                nc.scalar.activation(s["r2"][:, HALF:], s["r"][:, HALF:], ACT.Square)
             else:
-                for v in halves(k):
+                for v in halves(k) if k in TURNED else (slice(0, W),):
                     nc.scalar.activation(s["r2"][:, v], s["r"][:, v], ACT.Square)
 
         def variance(k, eng):
             s = st[k]
             s["var"] = temp(k, "var")
-            for v in halves(k):
-                eng.tensor_tensor(s["var"][:, v], s["u2"][:, v], s["r2"][:, v], ALU.add)
+            v = halves(k)[0]
+            eng.tensor_tensor(s["var"][:, v], s["u2"][:, v], s["r2"][:, v], ALU.add)
+
+        def variance_rest(k):
+            s = st[k]
+            v = halves(k)[1]
+            nc.vector.tensor_tensor(s["var"][:, v], s["u2"][:, v], s["r2"][:, v], ALU.add)
 
         def turn(k, target, tag, name, first):
             s = st[k]
@@ -243,12 +276,12 @@ def tile_picked_statpool_none_p_kernel(
             else:
                 nc.vector.tensor_scalar(target, s["sum"][:].rearrange("p t v -> p v t"), 1.0 / 3.0, None, ALU.mult)
 
-        def deviation(k, devs):
+        def deviation(k, devs, parts=slice(0, 2)):
             target = devs[:, k * W : (k + 1) * W]
             if k in TURNED:
                 nc.scalar.activation(woven(target), st[k]["var"][:].rearrange("p t v -> p v t"), ACT.Sqrt, scale=2.0 / 9.0, bias=floor[:])
             else:
-                for v in halves(k):
+                for v in halves(k)[parts]:
                     nc.scalar.activation(target[:, v], st[k]["var"][:, v], ACT.Sqrt, scale=1.0 / 18.0, bias=floor[:])
 
         mean_codes = keep.tile([P, V], U32, name="mean_codes", align_bytes=64)
@@ -290,7 +323,7 @@ def tile_picked_statpool_none_p_kernel(
         copy_h0(2)
         third(1)
         second(2)
-        copy_h0(3)
+        copy_turned(3)
         third(2)
         second(3)
         pair_of(0)
@@ -305,7 +338,7 @@ def tile_picked_statpool_none_p_kernel(
         third(3)
         square_r(1, False)
         square_u(2)
-        pair_of(3)
+        pair_turned(3)
         diff_r(2)
         variance(1, nc.gpsimd)
         square_r(2, False)
@@ -322,12 +355,14 @@ def tile_picked_statpool_none_p_kernel(
         mean_of(0, means)
         mean_of(1, means)
         mean_of(2, means)
-        mean_of(3, means)
+        variance_rest(2)
         quantize(means, mean_codes, mean_scales, 0, 2)
+        mean_of(3, means)
         deviation(0, devs)
         deviation(1, devs)
+        deviation(2, devs, slice(0, 1))
         deviation(3, devs)
-        deviation(2, devs)
+        deviation(2, devs, slice(1, 2))
         second_pass(0, 0)
         second_pass(1, 0)
         quantize(devs, dev_codes, dev_scales, 0, 2)

@@ -22,14 +22,14 @@ P = 128
 PACK = 4
 CHUNK = 128
 CHUNKS = V // CHUNK
-HALVED = (2, 3)
+HALVED = (3,)
 CUTS = (0, 80, 128)
 HALF = H // 2
 SHARE = 256
 SQRT_FLOOR = 2.0**-116
-TURNED = (3,)
-HOLDS = {(2, "pair"): "means", (3, "c0"): "devs"}
-ACCTAG = "abab"
+TURNED = (2,)
+HOLDS = {(3, "c0"): "means", (1, "pair"): "devs0", (1, "r2"): "devs1"}
+ACCTAG = "aaab"
 
 
 def tile_picked_statpool_none_p_kernel(
@@ -235,8 +235,7 @@ def tile_picked_statpool_none_p_kernel(
             s = st[k]
             s["r2"] = temp(k, "r2")
             if on_gpsimd:
-                nc.gpsimd.tensor_tensor(s["r2"][:, :HALF], s["r"][:, :HALF], s["r"][:, :HALF], ALU.mult)
-                nc.scalar.activation(s["r2"][:, HALF:], s["r"][:, HALF:], ACT.Square)
+                nc.gpsimd.tensor_tensor(s["r2"][:], s["r"][:], s["r"][:], ALU.mult)
             else:
                 for v in halves(k) if k in TURNED else (slice(0, W),):
                     nc.scalar.activation(s["r2"][:, v], s["r"][:, v], ACT.Square)
@@ -277,7 +276,7 @@ def tile_picked_statpool_none_p_kernel(
                 nc.vector.tensor_scalar(target, s["sum"][:].rearrange("p t v -> p v t"), 1.0 / 3.0, None, ALU.mult)
 
         def deviation(k, devs, parts=slice(0, 2)):
-            target = devs[:, k * W : (k + 1) * W]
+            target = devs[k // 2][:, k % 2 * W : (k % 2 + 1) * W]
             if k in TURNED:
                 nc.scalar.activation(woven(target), st[k]["var"][:].rearrange("p t v -> p v t"), ACT.Sqrt, scale=2.0 / 9.0, bias=floor[:])
             else:
@@ -289,9 +288,11 @@ def tile_picked_statpool_none_p_kernel(
         dev_codes = keep.tile([P, V], U32, name="dev_codes", align_bytes=64)
         dev_scales = keep.tile([P, V], U8, name="dev_scales", align_bytes=64)
 
-        def quantize(values, codes, scales, first, count):
+        def quantize(values, codes, scales, first, count, base=0):
             v = slice(first * CHUNK, (first + count) * CHUNK)
-            nc.vector.quantize_mx(out=codes[:, v].bitcast(FP8X4), scales=scales[:, v], in_=values[:, first * W : (first + count) * W])
+            nc.vector.quantize_mx(
+                out=codes[:, v].bitcast(FP8X4), scales=scales[:, v], in_=values[:, (first - base) * W : (first - base + count) * W]
+            )
 
         def second_pass(k, n):
             v = slice(k * CHUNK, (k + 1) * CHUNK)
@@ -320,12 +321,13 @@ def tile_picked_statpool_none_p_kernel(
         second(1)
         square_u(1)
         third(0)
-        copy_h0(2)
-        third(1)
+        copy_turned(2)
+        copy_h0(3)
         second(2)
-        copy_turned(3)
-        third(2)
+        third(1)
         second(3)
+        third(2)
+        third(3)
         pair_of(0)
         u_of_first()
         diff_r(0)
@@ -333,47 +335,45 @@ def tile_picked_statpool_none_p_kernel(
         square_u(0)
         square_r(0, True)
         variance(0, nc.gpsimd)
-        pair_of(2)
+        pair_turned(2)
         diff_r(1)
-        third(3)
-        square_r(1, False)
+        pair_of(3)
         square_u(2)
-        pair_turned(3)
+        square_r(1, False)
         diff_r(2)
         variance(1, nc.gpsimd)
         square_r(2, False)
-        variance(2, nc.gpsimd)
         square_u(3)
         diff_r(3)
         square_r(3, False)
-        turn(3, "sum", "b", "pair", True)
-        turn(3, "var", "a", "u2", True)
-        turn(3, "sum", "b", "r", False)
-        turn(3, "var", "a", "r2", False)
+        variance(3, nc.gpsimd)
+        turn(2, "sum", "b", "pair", True)
+        turn(2, "var", "b", "u2", True)
+        turn(2, "sum", "b", "r", False)
+        turn(2, "var", "b", "r2", False)
         means = keep.tile([P, CHUNKS * W], BF16, name="means", tag="means", align_bytes=64)
-        devs = keep.tile([P, CHUNKS * W], BF16, name="devs", tag="devs", align_bytes=64)
+        devs = [keep.tile([P, 2 * W], BF16, name=f"devs{n}", tag=f"devs{n}", align_bytes=64) for n in range(2)]
         mean_of(0, means)
         mean_of(1, means)
-        mean_of(2, means)
-        variance_rest(2)
-        quantize(means, mean_codes, mean_scales, 0, 2)
         mean_of(3, means)
+        mean_of(2, means)
+        variance_rest(3)
+        quantize(means, mean_codes, mean_scales, 0, 2)
         deviation(0, devs)
         deviation(1, devs)
-        deviation(2, devs, slice(0, 1))
+        deviation(2, devs)
         deviation(3, devs)
-        deviation(2, devs, slice(1, 2))
         second_pass(0, 0)
         second_pass(1, 0)
-        quantize(devs, dev_codes, dev_scales, 0, 2)
+        quantize(devs[0], dev_codes, dev_scales, 0, 2)
         second_pass(0, 1)
         second_pass(1, 1)
         quantize(means, mean_codes, mean_scales, 2, 2)
         second_pass(2, 0)
         second_pass(3, 0)
-        for k in (3, 2):
-            quantize(devs, dev_codes, dev_scales, k, 1)
+        for k in (2, 3):
+            quantize(devs[1], dev_codes, dev_scales, k, 1, 2)
             second_pass(k, 1)
         store((0, 1), nc.scalar.copy)
-        store((3,), nc.vector.tensor_copy)
         store((2,), nc.vector.tensor_copy)
+        store((3,), nc.vector.tensor_copy)

@@ -28,7 +28,7 @@ HALF = H // 2
 SHARE = 256
 SQRT_FLOOR = 2.0**-116
 TURNED = (2,)
-HOLDS = {(3, "c0"): "means", (1, "pair"): "devs0", (1, "r2"): "devs1"}
+HOLDS = {(3, "c0"): "means", (3, "pair"): "devs0", (1, "r2"): "devs1"}
 ACCTAG = "aaab"
 
 
@@ -114,8 +114,11 @@ def tile_picked_statpool_none_p_kernel(
             for r in range(4):
                 nc.sync.dma_start(w23_scales[r:P:32, n * N : (n + 1) * N].bitcast(I32), rows[r:16:4, :].bitcast(I32))
 
-        for d in range(3):
-            nc.vector.tensor_copy(xw[d][:], x_table[:].bitcast(U32).indirect(offsets[:, d * cols : (d + 1) * cols]))
+        words = x_table[:].bitcast(U32)
+        for g in range(2):
+            nc.vector.tensor_copy(xw[0][:, g * V // 2 : (g + 1) * V // 2], words.indirect(offsets[:, g * cols // 2 : (g + 1) * cols // 2]))
+        for d in (1, 2):
+            nc.vector.tensor_copy(xw[d][:], words.indirect(offsets[:, d * cols : (d + 1) * cols]))
 
         W = PACK * CHUNK
         last = CHUNKS - 1
@@ -317,12 +320,11 @@ def tile_picked_statpool_none_p_kernel(
 
         copy_h0(0)
         copy_h0(1)
-        second(0)
-        second(1)
-        square_u(1)
-        third(0)
-        copy_turned(2)
         copy_h0(3)
+        second(0)
+        copy_turned(2)
+        third(0)
+        second(1)
         second(2)
         third(1)
         second(3)
@@ -333,6 +335,7 @@ def tile_picked_statpool_none_p_kernel(
         diff_r(0)
         pair_of(1)
         square_u(0)
+        square_u(1)
         square_r(0, True)
         variance(0, nc.gpsimd)
         pair_turned(2)
@@ -342,8 +345,8 @@ def tile_picked_statpool_none_p_kernel(
         square_r(1, False)
         diff_r(2)
         variance(1, nc.gpsimd)
-        square_r(2, False)
         square_u(3)
+        square_r(2, False)
         diff_r(3)
         square_r(3, False)
         variance(3, nc.gpsimd)

@@ -335,8 +335,8 @@ def tile_picked_statpool_none_p_kernel(
         diff_r(0)
         pair_of(1)
         square_u(0)
+        square_r(0, False)
         square_u(1)
-        square_r(0, True)
         variance(0, nc.gpsimd)
         pair_turned(2)
         diff_r(1)

@@ -43,14 +43,14 @@ def tile_picked_statpool_none_p_kernel(
 
         offsets = keep.tile([P, S // 16], U16, name="offsets")
         xs_table = keep.tile([P, T], U8, name="xs_table", tag="scale_rows", align_bytes=64)
-        nc.gpsimd.memset(xs_table[:, : T // 2].bitcast(I32), 0)
-        nc.vector.memset(xs_table[:, T // 2 :].bitcast(I32), 0)
         one = keep.tile([P, 1], F32, name="one", tag="w1_raw1", align_bytes=64)
         unit = keep.tile([P, 1], F32, name="unit", tag="x_words", align_bytes=64)
         root_three = keep.tile([P, 1], F32, name="root_three")
         floor = keep.tile([P, 1], F32, name="floor")
-        nc.gpsimd.memset(one[:], 1.0)
-        nc.gpsimd.memset(unit[:], 1.0)
+        nc.vector.memset(one[:], 1.0)
+        nc.vector.memset(unit[:], 1.0)
+        nc.gpsimd.memset(xs_table[:, : T // 2].bitcast(I32), 0)
+        nc.vector.memset(xs_table[:, T // 2 :].bitcast(I32), 0)
         three = keep.tile([P, 1], F32, name="three")
         nc.vector.tensor_scalar(three[:], one[:], 3.0, None, ALU.mult)
         nc.vector.tensor_scalar(floor[:], unit[:], SQRT_FLOOR, None, ALU.mult)
@@ -65,7 +65,7 @@ def tile_picked_statpool_none_p_kernel(
 
         load_w1(0)
         nc.sync.dma_start(offsets[:], offs)
-        nc.scalar.dma_start(xs_table[0:P:8, :].bitcast(I32), x_scales[0].bitcast(I32))
+        nc.sync.dma_start(xs_table[0:P:8, :].bitcast(I32), x_scales[0].bitcast(I32))
         nc.scalar.activation(root_three[:], three[:], ACT.Sqrt)
         load_w1(1)
         x_table = keep.tile([P, T], I32, name="x_table", tag="x_words", align_bytes=64)

@@ -87,14 +87,15 @@ def tile_picked_statpool_none_p_kernel(
         nc.sync.dma_start(w3_codes.bitcast(I32), w3_words[0].bitcast(I32))
 
         identity = keep.tile([P, P], F32, name="identity")
-        make_identity(nc, identity[:])
+        nc.vector.memset(identity[:], 0.0)
+        make_identity(nc, identity[:], nomemset=True)
 
         cols = V // 16
         xs_all = keep.tile([P, S], U8, name="xs_all", align_bytes=64)
         xs = [xs_all[:, d * V : (d + 1) * V] for d in range(3)]
         xw = [keep.tile([P, V], U32, name=f"xw{d}", align_bytes=64) for d in range(3)]
         xs_picked = keep.tile([P, S], U8, name="xs_picked", align_bytes=64)
-        nc.gpsimd.memset(xs_all[:].bitcast(I32), 0)
+        nc.vector.memset(xs_all[:].bitcast(I32), 0)
         nc.vector.tensor_copy(xs_picked[:], xs_table[:].indirect(offsets[:]))
         for r in range(4):
             nc.sync.dma_start(xs_all[r:P:32, :].bitcast(I32), xs_picked[8 * r : P : 32, :].bitcast(I32))

@@ -23,9 +23,10 @@ PACK = 4
 CHUNK = 128
 CHUNKS = V // CHUNK
 HALVED = (3,)
-CUTS = (0, 80, 128)
+CUTS = (0, 72, 128)
+NEGATED = 1280
 HALF = H // 2
-SHARE = 256
+SHARE = 320
 SQRT_FLOOR = 2.0**-116
 TURNED = (2,)
 HOLDS = {(3, "c0"): "means", (3, "pair"): "devs0", (1, "r2"): "devs1"}
@@ -79,7 +80,7 @@ def tile_picked_statpool_none_p_kernel(
             )
         w1_flat = w1_bf[:].rearrange("p t m j -> p (t m j)")
         w1_minus = keep.tile([P, PACK * H], BF16, name="w1_minus", align_bytes=64)
-        nc.scalar.activation(w1_minus[:, : 2 * H], w1_flat[:, : 2 * H], ACT.Copy, scale=-1.0)
+        nc.scalar.activation(w1_minus[:, :NEGATED], w1_flat[:, :NEGATED], ACT.Copy, scale=-1.0)
         w23_codes = keep.tile([P, 4 * N], U8, name="w23_codes", tag="w1_raw0", align_bytes=64)
         w2_codes = w23_codes[:, 0 : 2 * N]
         w3_codes = w23_codes[:, 2 * N : 4 * N]
@@ -100,7 +101,7 @@ def tile_picked_statpool_none_p_kernel(
         for r in range(4):
             nc.sync.dma_start(xs_all[r:P:32, :].bitcast(I32), xs_picked[8 * r : P : 32, :].bitcast(I32))
 
-        nc.vector.tensor_scalar(w1_minus[:, 2 * H :], w1_flat[:, 2 * H :], -1.0, None, ALU.mult)
+        nc.vector.tensor_scalar(w1_minus[:, NEGATED:], w1_flat[:, NEGATED:], -1.0, None, ALU.mult)
         w1_codes = keep.tile([P, 2 * H], U32, name="w1_codes", align_bytes=64)
         w1_scales = keep.tile([P, 2 * H], U8, name="w1_scales", align_bytes=64)
         for sign, values in enumerate((w1_flat, w1_minus[:])):
@@ -232,7 +233,7 @@ def tile_picked_statpool_none_p_kernel(
         def square_u(k):
             s = st[k]
             s["u2"] = temp(k, "u2")
-            scale = math.sqrt(0.75) if k in TURNED else root_three[:]
+            scale = math.sqrt(0.75) if k in TURNED else root_three[:] if k == 0 else math.sqrt(3.0)
             nc.scalar.activation(laid(k, s["u2"]), s["u_bank"], ACT.Square, scale=scale)
 
         def square_r(k, on_gpsimd):
@@ -241,7 +242,7 @@ def tile_picked_statpool_none_p_kernel(
             if on_gpsimd:
                 nc.gpsimd.tensor_tensor(s["r2"][:], s["r"][:], s["r"][:], ALU.mult)
             else:
-                for v in halves(k) if k in TURNED else (slice(0, W),):
+                for v in halves(k):
                     nc.scalar.activation(s["r2"][:, v], s["r"][:, v], ACT.Square)
 
         def variance(k, eng):

import math
from contextlib import ExitStack

import concourse.mybir as mybir
from concourse.masks import make_identity

K, T, S, V, H, N = 512, 4096, 1536, 512, 512, 128
FLOPS = 2 * K * H * S + 2 * 2 * H * N * V

F32 = mybir.dt.float32
BF16 = mybir.dt.bfloat16
I32 = mybir.dt.int32
U32 = mybir.dt.uint32
U16 = mybir.dt.uint16
U8 = mybir.dt.uint8
FP8X4 = mybir.dt.float8_e4m3fn_x4
FP4X4 = mybir.dt.float4_e2m1fn_x4
ACT = mybir.ActivationFunctionType
ALU = mybir.AluOpType

P = 128
PACK = 4
CHUNK = 128
CHUNKS = V // CHUNK
HALVED = (3,)
CUTS = (0, 72, 128)
NEGATED = 1280
HALF = H // 2
SHARE = 320
SQRT_FLOOR = 2.0**-116
TURNED = (2,)
HOLDS = {(3, "c0"): "means", (3, "pair"): "devs0", (1, "r2"): "devs1"}
ACCTAG = "aaab"


def tile_picked_statpool_none_p_kernel(
    tc, x_words, x_scales, w1, w2_words, w2_scales, w3_words, w3_scales, offs, out
):
    nc = tc.nc
    with ExitStack() as ctx:
        keep = ctx.enter_context(tc.tile_pool(name="keep", bufs=1))
        work = ctx.enter_context(tc.tile_pool(name="work", bufs=4))
        psum = ctx.enter_context(tc.psum_pool(name="psum", bufs=2))

        offsets = keep.tile([P, S // 16], U16, name="offsets")
        xs_table = keep.tile([P, T], U8, name="xs_table", tag="scale_rows", align_bytes=64)
        one = keep.tile([P, 1], F32, name="one", tag="w1_raw1", align_bytes=64)
        unit = keep.tile([P, 1], F32, name="unit", tag="x_words", align_bytes=64)
        root_three = keep.tile([P, 1], F32, name="root_three")
        floor = keep.tile([P, 1], F32, name="floor")
        nc.vector.memset(one[:], 1.0)
        nc.vector.memset(unit[:], 1.0)
        nc.gpsimd.memset(xs_table[:, : T // 2].bitcast(I32), 0)
        nc.vector.memset(xs_table[:, T // 2 :].bitcast(I32), 0)
        three = keep.tile([P, 1], F32, name="three")
        nc.vector.tensor_scalar(three[:], one[:], 3.0, None, ALU.mult)
        nc.vector.tensor_scalar(floor[:], unit[:], SQRT_FLOOR, None, ALU.mult)

        w1_rows = w1.rearrange("(p j) c -> p j c", j=PACK)
        w1_raw = []

        def load_w1(g):
            raw = keep.tile([P, PACK, PACK * (CUTS[g + 1] - CUTS[g])], F32, name=f"w1_raw{g}", align_bytes=64)
            nc.sync.dma_start(raw[:], w1_rows[:, :, PACK * CUTS[g] : PACK * CUTS[g + 1]])
            w1_raw.append(raw)

        load_w1(0)
        nc.sync.dma_start(offsets[:], offs)
        nc.sync.dma_start(xs_table[0:P:8, :].bitcast(I32), x_scales[0].bitcast(I32))
        nc.scalar.activation(root_three[:], three[:], ACT.Sqrt)
        load_w1(1)
        x_table = keep.tile([P, T], I32, name="x_table", tag="x_words", align_bytes=64)
        nc.sync.dma_start(x_table[:], x_words[0].rearrange("p n t -> p (n t)").bitcast(I32))

        w1_bf = keep.tile([P, PACK, P, PACK], BF16, name="w1_bf", tag="w1_bf", align_bytes=64)
        for g in range(2):
            nc.scalar.copy(
                w1_bf[:, :, CUTS[g] : CUTS[g + 1], :].rearrange("p t m j -> p m t j"),
                w1_raw[g][:].rearrange("p j (m t) -> p m t j", t=PACK),
            )
        w1_flat = w1_bf[:].rearrange("p t m j -> p (t m j)")
        w1_minus = keep.tile([P, PACK * H], BF16, name="w1_minus", align_bytes=64)
        nc.scalar.activation(w1_minus[:, :NEGATED], w1_flat[:, :NEGATED], ACT.Copy, scale=-1.0)
        w23_codes = keep.tile([P, 4 * N], U8, name="w23_codes", tag="w1_raw0", align_bytes=64)
        w2_codes = w23_codes[:, 0 : 2 * N]
        w3_codes = w23_codes[:, 2 * N : 4 * N]
        nc.sync.dma_start(w2_codes.bitcast(I32), w2_words[0].bitcast(I32))
        nc.sync.dma_start(w3_codes.bitcast(I32), w3_words[0].bitcast(I32))

        identity = keep.tile([P, P], F32, name="identity")
        nc.vector.memset(identity[:], 0.0)
        make_identity(nc, identity[:], nomemset=True)

        cols = V // 16
        xs_all = keep.tile([P, S], U8, name="xs_all", align_bytes=64)
        xs = [xs_all[:, d * V : (d + 1) * V] for d in range(3)]
        xw = [keep.tile([P, V], U32, name=f"xw{d}", align_bytes=64) for d in range(3)]
        xs_picked = keep.tile([P, S], U8, name="xs_picked", align_bytes=64)
        nc.vector.memset(xs_all[:].bitcast(I32), 0)
        nc.vector.tensor_copy(xs_picked[:], xs_table[:].indirect(offsets[:]))
        for r in range(4):
            nc.sync.dma_start(xs_all[r:P:32, :].bitcast(I32), xs_picked[8 * r : P : 32, :].bitcast(I32))

        nc.vector.tensor_scalar(w1_minus[:, NEGATED:], w1_flat[:, NEGATED:], -1.0, None, ALU.mult)
        w1_codes = keep.tile([P, 2 * H], U32, name="w1_codes", align_bytes=64)
        w1_scales = keep.tile([P, 2 * H], U8, name="w1_scales", align_bytes=64)
        for sign, values in enumerate((w1_flat, w1_minus[:])):
            nc.vector.quantize_mx(
                out=w1_codes[:, sign * H : (sign + 1) * H].bitcast(FP8X4),
                scales=w1_scales[:, sign * H : (sign + 1) * H],
                in_=values,
            )
        w23_scales = keep.tile([P, 2 * N], U8, name="w23_scales", tag="w1_bf", align_bytes=64)
        nc.vector.memset(w23_scales[:].bitcast(I32), 0)
        for n, rows in enumerate((w2_scales[0], w3_scales[0])):
            for r in range(4):
                nc.sync.dma_start(w23_scales[r:P:32, n * N : (n + 1) * N].bitcast(I32), rows[r:16:4, :].bitcast(I32))

        words = x_table[:].bitcast(U32)
        for g in range(2):
            nc.vector.tensor_copy(xw[0][:, g * V // 2 : (g + 1) * V // 2], words.indirect(offsets[:, g * cols // 2 : (g + 1) * cols // 2]))
        for d in (1, 2):
            nc.vector.tensor_copy(xw[d][:], words.indirect(offsets[:, d * cols : (d + 1) * cols]))

        W = PACK * CHUNK
        last = CHUNKS - 1
        st = [dict() for k in range(CHUNKS)]

        def woven(tile):
            return tile[:].rearrange("p (v t) -> p v t", t=PACK)

        def first_product(tag, pieces, k):
            v = slice(k * CHUNK, (k + 1) * CHUNK)
            bank = psum.tile([P, H], F32, name=tag, bufs=CHUNKS)
            if k in TURNED:
                for n, (d, sign) in enumerate(pieces):
                    m = slice(sign * H, (sign + 1) * H)
                    nc.tensor.matmul_mx(
                        out=bank[:],
                        lhsT=xw[d][:, v].bitcast(FP8X4),
                        lhsT_scale=xs[d][:, v],
                        rhs=w1_codes[:, m].bitcast(FP8X4),
                        rhs_scale=w1_scales[:, m],
                        start=(n == 0),
                        stop=(n == len(pieces) - 1),
                    )
                return bank[:]
            for t in range(PACK):
                for n, (d, sign) in enumerate(pieces):
                    m = slice(sign * H + t * P, sign * H + (t + 1) * P)
                    nc.tensor.matmul_mx(
                        out=bank[:, t * CHUNK : (t + 1) * CHUNK],
                        lhsT=w1_codes[:, m].bitcast(FP8X4),
                        lhsT_scale=w1_scales[:, m],
                        rhs=xw[d][:, v].bitcast(FP8X4),
                        rhs_scale=xs[d][:, v],
                        start=(n == 0),
                        stop=(n == len(pieces) - 1),
                    )
            return bank[:].rearrange("p (t v) -> p v t", t=PACK)

        def halves(k):
            cut = W // 2 if k in TURNED else SHARE
            return (slice(0, cut), slice(cut, W)) if k in HALVED else (slice(0, W),)

        def laid(k, tile):
            return tile[:] if k in TURNED else woven(tile)

        def temp(k, name):
            if (k, name) in HOLDS:
                return keep.tile([P, W], F32, name=f"late_{name}", tag=HOLDS[(k, name)], align_bytes=64)
            return work.tile([P, W], F32, name=name)

        def copy_h0(k):
            s = st[k]
            s["c0"] = temp(k, "c0")
            nc.scalar.activation(laid(k, s["c0"]), first_product("a", ((0, 0),), k), ACT.Copy, scale=3.0 if k in TURNED else 2.0)

        def copy_turned(k):
            s = st[k]
            v = slice(k * CHUNK, (k + 1) * CHUNK)
            bank = psum.tile([P, H], F32, name="a", bufs=CHUNKS)
            for m, pieces in ((slice(0, HALF), (0, 1)), (slice(HALF, H), (0,))):
                for n, d in enumerate(pieces):
                    nc.tensor.matmul_mx(
                        out=bank[:, m],
                        lhsT=xw[d][:, v].bitcast(FP8X4),
                        lhsT_scale=xs[d][:, v],
                        rhs=w1_codes[:, m].bitcast(FP8X4),
                        rhs_scale=w1_scales[:, m],
                        start=(n == 0),
                        stop=(n == len(pieces) - 1),
                    )
            s["c0"] = temp(k, "c0")
            s["pair"] = keep.tile([P, W], F32, name="pair_turned")
            nc.scalar.activation(s["c0"][:, HALF:], bank[:, HALF:], ACT.Copy, scale=3.0)
            nc.scalar.activation(s["pair"][:, :HALF], bank[:, :HALF], ACT.Copy, scale=1.5)

        def pair_turned(k):
            s = st[k]
            nc.vector.scalar_tensor_tensor(s["pair"][:, HALF:], s["u_bank"][:, HALF:], 1.5, s["c0"][:, HALF:], ALU.mult, ALU.add)

        def second(k):
            st[k]["u_bank"] = first_product("b", ((1, 0),) if k == 0 else ((1, 0), (0, 1)), k)

        def third(k):
            st[k]["h2"] = first_product("a", ((2, 0),), k)

        def pair_of(k):
            s = st[k]
            s["pair"] = temp(k, "pair")
            if k == 0:
                nc.vector.scalar_tensor_tensor(woven(s["pair"]), woven(s["c0"]), 0.5, s["u_bank"], ALU.mult, ALU.add)
            else:
                nc.vector.scalar_tensor_tensor(
                    laid(k, s["pair"]), s["u_bank"], 1.5 if k in TURNED else 1.0, laid(k, s["c0"]), ALU.mult, ALU.add
                )

        def u_of_first():
            s = st[0]
            u = temp(0, "u")
            nc.vector.scalar_tensor_tensor(woven(u), woven(s["c0"]), -0.5, s["u_bank"], ALU.mult, ALU.add)
            s["u_bank"] = woven(u)

        def diff_r(k):
            s = st[k]
            s["r"] = temp(k, "r")
            if k in TURNED:
                nc.vector.scalar_tensor_tensor(s["r"][:], s["pair"][:], -1.0 / 3.0, s["h2"], ALU.mult, ALU.add)
            else:
                nc.vector.scalar_tensor_tensor(woven(s["r"]), s["h2"], 2.0, woven(s["pair"]), ALU.mult, ALU.subtract)

        def square_u(k):
            s = st[k]
            s["u2"] = temp(k, "u2")
            scale = math.sqrt(0.75) if k in TURNED else root_three[:] if k == 0 else math.sqrt(3.0)
            nc.scalar.activation(laid(k, s["u2"]), s["u_bank"], ACT.Square, scale=scale)

        def square_r(k, on_gpsimd):
            s = st[k]
            s["r2"] = temp(k, "r2")
            if on_gpsimd:
                nc.gpsimd.tensor_tensor(s["r2"][:], s["r"][:], s["r"][:], ALU.mult)
            else:
                for v in halves(k):
                    nc.scalar.activation(s["r2"][:, v], s["r"][:, v], ACT.Square)

        def variance(k, eng):
            s = st[k]
            s["var"] = temp(k, "var")
            v = halves(k)[0]
            eng.tensor_tensor(s["var"][:, v], s["u2"][:, v], s["r2"][:, v], ALU.add)

        def variance_rest(k):
            s = st[k]
            v = halves(k)[1]
            nc.vector.tensor_tensor(s["var"][:, v], s["u2"][:, v], s["r2"][:, v], ALU.add)

        def turn(k, target, tag, name, first):
            s = st[k]
            if first:
                s[target] = psum.tile([P, PACK, CHUNK], F32, name=tag, bufs=CHUNKS)
            for t in range(PACK):
                nc.tensor.matmul(
                    s[target][:, t, :],
                    s[name][:, t * P : (t + 1) * P],
                    identity[:],
                    is_transpose=True,
                    start=first and t == 0,
                    stop=not first and t == PACK - 1,
                )

        def mean_of(k, means, on_scalar=False):
            s = st[k]
            target = woven(means[:, k * W : (k + 1) * W])
            if k not in TURNED:
                nc.vector.scalar_tensor_tensor(target, woven(s["r"]), -1.0 / 3.0, s["h2"], ALU.mult, ALU.add)
            elif on_scalar:
                nc.scalar.activation(target, s["sum"][:].rearrange("p t v -> p v t"), ACT.Copy, scale=1.0 / 3.0)
            else:
                nc.vector.tensor_scalar(target, s["sum"][:].rearrange("p t v -> p v t"), 1.0 / 3.0, None, ALU.mult)

        def deviation(k, devs, parts=slice(0, 2)):
            target = devs[k // 2][:, k % 2 * W : (k % 2 + 1) * W]
            if k in TURNED:
                nc.scalar.activation(woven(target), st[k]["var"][:].rearrange("p t v -> p v t"), ACT.Sqrt, scale=2.0 / 9.0, bias=floor[:])
            else:
                for v in halves(k)[parts]:
                    nc.scalar.activation(target[:, v], st[k]["var"][:, v], ACT.Sqrt, scale=1.0 / 18.0, bias=floor[:])

        mean_codes = keep.tile([P, V], U32, name="mean_codes", align_bytes=64)
        mean_scales = keep.tile([P, V], U8, name="mean_scales", align_bytes=64)
        dev_codes = keep.tile([P, V], U32, name="dev_codes", align_bytes=64)
        dev_scales = keep.tile([P, V], U8, name="dev_scales", align_bytes=64)

        def quantize(values, codes, scales, first, count, base=0):
            v = slice(first * CHUNK, (first + count) * CHUNK)
            nc.vector.quantize_mx(
                out=codes[:, v].bitcast(FP8X4), scales=scales[:, v], in_=values[:, (first - base) * W : (first - base + count) * W]
            )

        def second_pass(k, n):
            v = slice(k * CHUNK, (k + 1) * CHUNK)
            if n == 0:
                st[k]["acc"] = psum.tile([P, CHUNK], F32, name=ACCTAG[k], bufs=CHUNKS)
            codes, vals, scales = ((w2_codes, mean_codes, mean_scales), (w3_codes, dev_codes, dev_scales))[n]
            nc.tensor.matmul_mx(
                out=st[k]["acc"][:],
                lhsT=codes.bitcast(FP4X4),
                lhsT_scale=w23_scales[:, n * N : (n + 1) * N],
                rhs=vals[:, v].bitcast(FP8X4),
                rhs_scale=scales[:, v],
                start=(n == 0),
                stop=(n == 1),
            )

        def store(chunks, copy):
            res = work.tile([P, len(chunks) * CHUNK], F32, name="res")
            for place, k in enumerate(chunks):
                copy(res[:, place * CHUNK : (place + 1) * CHUNK], st[k]["acc"][:])
            nc.sync.dma_start(out[:, chunks[0] * CHUNK : (chunks[-1] + 1) * CHUNK], res[:])

        copy_h0(0)
        copy_h0(1)
        copy_h0(3)
        second(0)
        copy_turned(2)
        third(0)
        second(1)
        second(2)
        third(1)
        second(3)
        third(2)
        third(3)
        pair_of(0)
        u_of_first()
        diff_r(0)
        pair_of(1)
        square_u(0)
        square_r(0, False)
        square_u(1)
        variance(0, nc.gpsimd)
        pair_turned(2)
        diff_r(1)
        pair_of(3)
        square_u(2)
        square_r(1, False)
        diff_r(2)
        variance(1, nc.gpsimd)
        square_u(3)
        square_r(2, False)
        diff_r(3)
        square_r(3, False)
        variance(3, nc.gpsimd)
        turn(2, "sum", "b", "pair", True)
        turn(2, "var", "b", "u2", True)
        turn(2, "sum", "b", "r", False)
        turn(2, "var", "b", "r2", False)
        means = keep.tile([P, CHUNKS * W], BF16, name="means", tag="means", align_bytes=64)
        devs = [keep.tile([P, 2 * W], BF16, name=f"devs{n}", tag=f"devs{n}", align_bytes=64) for n in range(2)]
        mean_of(0, means)
        mean_of(1, means)
        mean_of(3, means)
        mean_of(2, means)
        variance_rest(3)
        quantize(means, mean_codes, mean_scales, 0, 2)
        deviation(0, devs)
        deviation(1, devs)
        deviation(2, devs)
        deviation(3, devs)
        second_pass(0, 0)
        second_pass(1, 0)
        quantize(devs[0], dev_codes, dev_scales, 0, 2)
        second_pass(0, 1)
        second_pass(1, 1)
        quantize(means, mean_codes, mean_scales, 2, 2)
        second_pass(2, 0)
        second_pass(3, 0)
        for k in (2, 3):
            quantize(devs[1], dev_codes, dev_scales, k, 1, 2)
            second_pass(k, 1)
        store((0, 1), nc.scalar.copy)
        store((2,), nc.vector.tensor_copy)
        store((3,), nc.vector.tensor_copy)
